import numpy as np
import ml_dtypes


def mxq(x, axis, fmt="e4m3"):
    dtype, down = {"e4m3": (ml_dtypes.float8_e4m3fn, 7), "e5m2": (ml_dtypes.float8_e5m2, 14)}[fmt]
    v = np.moveaxis(np.asarray(x, np.float32).astype(ml_dtypes.bfloat16).astype(np.float64), axis, -1)
    blocks = v.reshape(v.shape[:-1] + (-1, 32))
    amax = np.abs(blocks).max(-1, keepdims=True)
    byte = np.maximum(np.where(amax > 0, np.frexp(amax)[1] - 1 + 127, 0) - down, 1)
    scale = np.exp2(byte - 127.0)
    codes = (blocks / scale).astype(np.float32).astype(dtype).astype(np.float64)
    return np.moveaxis((codes * scale).reshape(v.shape), -1, axis)


WIDE = False


def mx_kscale(k):
    if not WIDE:
        return np.ones(k)
    levels = np.array([30, -30])
    if k % 512:
        return np.exp2(np.random.permutation(np.resize(levels, k // 32))).repeat(32)
    a = np.empty((k // 512, 16))
    for p in range(k // 512):
        a[p, :8] = np.random.permutation(np.resize(levels, 8))
        for g in range(8):
            far = levels[np.abs(levels - a[p, g]) >= 10]
            a[p, g + 8] = far[np.random.randint(len(far))]
    return np.exp2(a.ravel()).repeat(32)


def f64(x):
    return np.asarray(x).astype(np.float64)


E2M1 = np.array([0.0, 0.5, 1.0, 1.5, 2.0, 3.0, 4.0, 6.0, -0.0, -0.5, -1.0, -1.5, -2.0, -3.0, -4.0, -6.0])


def pack_weight(w, fmt):
    k, n = w.shape
    w = f64(np.asarray(w, np.float32).astype(ml_dtypes.bfloat16)).reshape(k // 32, 32, n)
    amax = np.abs(w).max(1)
    if fmt == "e4m3":
        byte = np.frexp(amax)[1] - 1 + 127 - 7
    else:
        mant, ex = np.frexp(amax / 6.0)
        byte = np.where(mant > 0.5, ex, ex - 1) + 127
    byte = np.clip(np.where(amax > 0, byte, 1), 1, 254)
    scaled = (w * np.exp2(127.0 - byte)[:, None, :]).reshape(k, n).astype(np.float32)
    by_word = np.ascontiguousarray(scaled.reshape(k // 512, 128, 4, n).transpose(0, 1, 3, 2))
    if fmt == "e4m3":
        words = by_word.astype(ml_dtypes.float8_e4m3fn).view(np.uint8)
    else:
        c = by_word.astype(ml_dtypes.float4_e2m1fn).view(np.uint8) & 0xF
        words = (c[..., 0::2] | (c[..., 1::2] << 4)).reshape(k // 512, 128, 2 * n)
    return np.ascontiguousarray(words), np.ascontiguousarray(byte.astype(np.uint8).reshape(k // 512, 16, n))


def unpack_weight(words, scales, fmt):
    g, _, n = scales.shape
    words = np.ascontiguousarray(words).reshape(g, 128, n, -1)
    if fmt == "e4m3":
        vals = words.view(ml_dtypes.float8_e4m3fn).astype(np.float64)
    else:
        nib = np.empty((g, 128, n, 4), np.uint8)
        nib[..., 0::2] = words & 0xF
        nib[..., 1::2] = words >> 4
        vals = E2M1[nib]
    vals = vals * np.repeat(np.exp2(scales.astype(np.float64) - 127.0), 8, axis=1)[..., None]
    return vals.transpose(0, 1, 3, 2).reshape(g * 512, n)


N, R, K, T = 1536, 512, 1536, 512


def setup_inputs():
    n = np.random.standard_normal
    s = mx_kscale(N)[:, None]
    u = mx_kscale(R)[:, None]
    m = np.exp(0.5 * n((1, T)))
    p_w8 = pack_weight(n((N, K)) / np.sqrt(N) / s, "e4m3")
    return {
        "dy": (m * n((N, T)) * s).astype(np.float32),
        "w8_words": p_w8[0],
        "w8_scales": p_w8[1],
        "bu": (n((N, R)) / np.sqrt(N) / s * u.T).astype(np.float32),
        "ad": (0.5 * n((R, K)) / np.sqrt(R) / u).astype(np.float32),
        "res": (n((K, T))).astype(np.float32),
    }


def reference(dy, w8_words, w8_scales, bu, ad, res):
    dy_ = mxq(f64(dy), 0, "e5m2")
    w8_ = unpack_weight(w8_words, w8_scales, "e4m3")
    bu_ = mxq(f64(bu), 0, "e4m3")
    h = bu_.T @ dy_
    h_ = mxq(h, 0, "e5m2")
    ad_ = mxq(f64(ad), 0, "e4m3")
    dx = w8_.T @ dy_ + ad_.T @ h_
    return f64(res) + dx, h

@@ -1,0 +1,148 @@
+from contextlib import ExitStack
+
+import concourse.mybir as mybir
+
+N, R, K, T = 1536, 512, 1536, 512
+FLOPS = 2 * T * (N * R + N * K + R * K)
+
+F32 = mybir.dt.float32
+BF16 = mybir.dt.bfloat16
+I32 = mybir.dt.int32
+U32 = mybir.dt.uint32
+U8 = mybir.dt.uint8
+E4M3 = mybir.dt.float8_e4m3fn_x4
+E5M2 = mybir.dt.float8_e5m2_x4
+
+P = 128
+PACK = 4
+K_PASS = P * PACK
+PASSES = N // K_PASS
+WIDE = 512
+CHUNKS = K // WIDE
+TILES = WIDE // P
+SCALAR_COLS = 192
+
+
+def tile_mix_lrbwd_res_kernel(tc, dy, w8_words, w8_scales, bu, ad, res, out_0, out_1):
+    nc = tc.nc
+
+    with ExitStack() as ctx:
+        keep = ctx.enter_context(tc.tile_pool(name="keep", bufs=1))
+        stage = ctx.enter_context(tc.tile_pool(name="stage", bufs=3))
+        psum = ctx.enter_context(tc.psum_pool(name="psum", bufs=1))
+        ctx.enter_context(tc.manual_schedule())
+
+        def load_rows(name, rows):
+            raw = keep.tile([P, PACK, WIDE], F32, name=name)
+            nc.sync.dma_start(out=raw[:], in_=rows.rearrange("(p j) w -> p j w", j=PACK))
+            return raw
+
+        def quantize(name, grouped, fmt):
+            codes = keep.tile([P, WIDE], U32, name=name + "_codes", align_bytes=64)
+            scales = keep.tile([P, WIDE], U8, name=name + "_scales", align_bytes=64)
+            nc.vector.quantize_mx(out=codes[:].bitcast(fmt), scales=scales[:], in_=grouped[:])
+            return codes, scales
+
+        def interleave(raw):
+            grouped = stage.tile([P, WIDE * PACK], BF16, name="grouped", align_bytes=64)
+            dst = grouped[:].rearrange("p (c i j) -> p c j i", i=4, j=PACK)
+            src = raw[:].rearrange("p j (c i) -> p c j i", i=4)
+            cut = SCALAR_COLS // 4
+            nc.scalar.copy(out=dst[:, :cut], in_=src[:, :cut])
+            nc.vector.tensor_copy(out=dst[:, cut:], in_=src[:, cut:])
+            return grouped
+
+        def interleave_permuted(raw):
+            grouped = stage.tile([P, WIDE * PACK], BF16, name="grouped", align_bytes=64)
+            dst = grouped[:].rearrange("p (s m j) -> p m s j", s=PACK, j=PACK)
+            src = raw[:].rearrange("p j (m s) -> p m s j", s=PACK)
+            cut = SCALAR_COLS // 4
+            nc.scalar.copy(out=dst[:, :cut], in_=src[:, :cut])
+            nc.vector.tensor_copy(out=dst[:, cut:], in_=src[:, cut:])
+            return grouped
+
+        def mx_pass(acc, lhs, cols, rhs, start, stop):
+            nc.tensor.matmul_mx(
+                out=acc[:],
+                lhsT=lhs[0][:, cols].bitcast(E4M3),
+                lhsT_scale=lhs[1][:, cols],
+                rhs=rhs[0][:].bitcast(E5M2),
+                rhs_scale=rhs[1][:],
+                start=start,
+                stop=stop,
+            )
+
+        def bank(b):
+            acc = psum.tile([P, WIDE], F32, name="bank%d" % b)
+            return acc
+
+        w_plane = keep.tile([P, PASSES * K], U8, name="w_plane", align_bytes=64)
+        nc.vector.memset(w_plane[:].bitcast(I32), 0)
+
+        dy_raw = [load_rows("dy_raw0", dy[0:K_PASS, :])]
+        for q in range(4):
+            nc.sync.dma_start(
+                out=w_plane[32 * q : 32 * q + 4, :].bitcast(I32).rearrange("r (a n) -> r a n", a=PASSES),
+                in_=w8_scales[:, 4 * q : 4 * q + 4, :].bitcast(I32).rearrange("a r n -> r a n"),
+            )
+        for a in range(1, PASSES):
+            dy_raw.append(load_rows("dy_raw%d" % a, dy[a * K_PASS : (a + 1) * K_PASS, :]))
+        bu_raw = [load_rows("bu_raw%d" % a, bu[a * K_PASS : (a + 1) * K_PASS, :]) for a in range(PASSES)]
+        w_q = []
+        for a in range(PASSES):
+            w_codes = keep.tile([P, K], U32, name="w_codes%d" % a, align_bytes=64)
+            nc.sync.dma_start(
+                out=w_codes[:].bitcast(I32),
+                in_=w8_words[a].rearrange("p n i -> p (n i)").bitcast(I32),
+            )
+            w_q.append((w_codes, w_plane[:, a * K : (a + 1) * K]))
+        ad_raw = []
+        sums = []
+        for c in range(CHUNKS):
+            ad_raw.append(load_rows("ad_raw%d" % c, ad[:, c * WIDE : (c + 1) * WIDE]))
+            res_sb = keep.tile([P, TILES, T], F32, name="res%d" % c)
+            nc.sync.dma_start(out=res_sb[:], in_=res[c * WIDE : (c + 1) * WIDE, :].rearrange("(i p) t -> p i t", p=P))
+            sums.append(res_sb)
+
+        dy_q = [quantize("dy%d" % a, interleave(dy_raw[a]), E5M2) for a in range(PASSES)]
+        h_acc = [bank(s) for s in range(PACK)]
+        for a in range(PASSES):
+            bu_q = quantize("bu%d" % a, interleave_permuted(bu_raw[a]), E4M3)
+            for s in range(PACK):
+                mx_pass(h_acc[s], bu_q, slice(s * P, (s + 1) * P), dy_q[a], a == 0, a == PASSES - 1)
+        h_sb = keep.tile([P, PACK, T], F32, name="h_sb")
+        for s in range(PACK):
+            if s % 2 == 0:
+                nc.scalar.copy(out=h_sb[:, s, :], in_=h_acc[s][:])
+            else:
+                nc.vector.tensor_copy(out=h_sb[:, s, :], in_=h_acc[s][:])
+        h_q = quantize("h", interleave(h_sb), E5M2)
+        nc.sync.dma_start(out=out_1.rearrange("(p j) t -> p j t", j=PACK), in_=h_sb[:])
+
+        acc = {}
+
+        def base(chunks):
+            for c in chunks:
+                for i in range(TILES):
+                    acc[c, i] = bank(TILES * ((c + 1) % 2) + i)
+            for a in range(PASSES):
+                for c in chunks:
+                    for i in range(TILES):
+                        k0 = c * WIDE + i * P
+                        mx_pass(acc[c, i], w_q[a], slice(k0, k0 + P), dy_q[a], a == 0, False)
+
+        def finish(c):
+            ad_q = quantize("ad%d" % c, interleave(ad_raw[c]), E4M3)
+            for i in range(TILES):
+                mx_pass(acc[c, i], ad_q, slice(i * P, (i + 1) * P), h_q, False, True)
+            for i in range(TILES):
+                nc.vector.tensor_tensor(out=sums[c][:, i, :], in0=acc[c, i][:], in1=sums[c][:, i, :], op=mybir.AluOpType.add)
+            nc.sync.dma_start(
+                out=out_0[c * WIDE : (c + 1) * WIDE, :].rearrange("(i p) t -> p i t", p=P), in_=sums[c][:]
+            )
+
+        base([0, 1])
+        finish(0)
+        base([2])
+        finish(1)
+        finish(2)

@@ -21,6 +21,7 @@ WIDE = 512
 CHUNKS = K // WIDE
 TILES = WIDE // P
 SCALAR_COLS = 192
+SCALAR_COLS_AD = 256
 
 
 def tile_mix_lrbwd_res_kernel(tc, dy, w8_words, w8_scales, bu, ad, res, out_0, out_1):
@@ -33,7 +34,7 @@ def tile_mix_lrbwd_res_kernel(tc, dy, w8_words, w8_scales, bu, ad, res, out_0, o
         ctx.enter_context(tc.manual_schedule())
 
         def load_rows(name, rows):
-            raw = keep.tile([P, PACK, WIDE], F32, name=name)
+            raw = keep.tile([P, PACK, rows.shape[1]], F32, name=name)
             nc.sync.dma_start(out=raw[:], in_=rows.rearrange("(p j) w -> p j w", j=PACK))
             return raw
 
@@ -43,11 +44,11 @@ def tile_mix_lrbwd_res_kernel(tc, dy, w8_words, w8_scales, bu, ad, res, out_0, o
             nc.vector.quantize_mx(out=codes[:].bitcast(fmt), scales=scales[:], in_=grouped[:])
             return codes, scales
 
-        def interleave(raw):
+        def interleave(raw, scalar_cols):
             grouped = stage.tile([P, WIDE * PACK], BF16, name="grouped", align_bytes=64)
             dst = grouped[:].rearrange("p (c i j) -> p c j i", i=4, j=PACK)
-            src = raw[:].rearrange("p j (c i) -> p c j i", i=4)
-            cut = SCALAR_COLS // 4
+            src = raw.rearrange("p j (c i) -> p c j i", i=4)
+            cut = scalar_cols // 4
             nc.scalar.copy(out=dst[:, :cut], in_=src[:, :cut])
             nc.vector.tensor_copy(out=dst[:, cut:], in_=src[:, cut:])
             return grouped
@@ -79,32 +80,30 @@ def tile_mix_lrbwd_res_kernel(tc, dy, w8_words, w8_scales, bu, ad, res, out_0, o
         w_plane = keep.tile([P, PASSES * K], U8, name="w_plane", align_bytes=64)
         nc.vector.memset(w_plane[:].bitcast(I32), 0)
 
-        dy_raw = [load_rows("dy_raw0", dy[0:K_PASS, :])]
-        for q in range(4):
-            nc.sync.dma_start(
-                out=w_plane[32 * q : 32 * q + 4, :].bitcast(I32).rearrange("r (a n) -> r a n", a=PASSES),
-                in_=w8_scales[:, 4 * q : 4 * q + 4, :].bitcast(I32).rearrange("a r n -> r a n"),
+        for r in range(4):
+            nc.gpsimd.dma_start(
+                out=w_plane[r:P:32, :].bitcast(I32).rearrange("q (a n) -> q a n", a=PASSES),
+                in_=w8_scales[:, r:16:4, :].bitcast(I32).rearrange("a q n -> q a n"),
             )
-        for a in range(1, PASSES):
-            dy_raw.append(load_rows("dy_raw%d" % a, dy[a * K_PASS : (a + 1) * K_PASS, :]))
+        dy_raw = [load_rows("dy_raw%d" % a, dy[a * K_PASS : (a + 1) * K_PASS, :]) for a in range(PASSES)]
         bu_raw = [load_rows("bu_raw%d" % a, bu[a * K_PASS : (a + 1) * K_PASS, :]) for a in range(PASSES)]
         w_q = []
         for a in range(PASSES):
+            if a == PASSES - 1:
+                ad_raw = load_rows("ad_raw", ad)
             w_codes = keep.tile([P, K], U32, name="w_codes%d" % a, align_bytes=64)
             nc.sync.dma_start(
                 out=w_codes[:].bitcast(I32),
                 in_=w8_words[a].rearrange("p n i -> p (n i)").bitcast(I32),
             )
             w_q.append((w_codes, w_plane[:, a * K : (a + 1) * K]))
-        ad_raw = []
         sums = []
         for c in range(CHUNKS):
-            ad_raw.append(load_rows("ad_raw%d" % c, ad[:, c * WIDE : (c + 1) * WIDE]))
             res_sb = keep.tile([P, TILES, T], F32, name="res%d" % c)
             nc.sync.dma_start(out=res_sb[:], in_=res[c * WIDE : (c + 1) * WIDE, :].rearrange("(i p) t -> p i t", p=P))
             sums.append(res_sb)
 
-        dy_q = [quantize("dy%d" % a, interleave(dy_raw[a]), E5M2) for a in range(PASSES)]
+        dy_q = [quantize("dy%d" % a, interleave(dy_raw[a][:], SCALAR_COLS), E5M2) for a in range(PASSES)]
         h_acc = [bank(s) for s in range(PACK)]
         for a in range(PASSES):
             bu_q = quantize("bu%d" % a, interleave_permuted(bu_raw[a]), E4M3)
@@ -116,33 +115,47 @@ def tile_mix_lrbwd_res_kernel(tc, dy, w8_words, w8_scales, bu, ad, res, out_0, o
                 nc.scalar.copy(out=h_sb[:, s, :], in_=h_acc[s][:])
             else:
                 nc.vector.tensor_copy(out=h_sb[:, s, :], in_=h_acc[s][:])
-        h_q = quantize("h", interleave(h_sb), E5M2)
+        h_q = quantize("h", interleave(h_sb[:], SCALAR_COLS), E5M2)
         nc.sync.dma_start(out=out_1.rearrange("(p j) t -> p j t", j=PACK), in_=h_sb[:])
 
         acc = {}
 
-        def base(chunks):
-            for c in chunks:
-                for i in range(TILES):
-                    acc[c, i] = bank(TILES * ((c + 1) % 2) + i)
-            for a in range(PASSES):
-                for c in chunks:
-                    for i in range(TILES):
-                        k0 = c * WIDE + i * P
-                        mx_pass(acc[c, i], w_q[a], slice(k0, k0 + P), dy_q[a], a == 0, False)
+        def open_banks(c):
+            for i in range(TILES):
+                acc[c, i] = bank(TILES * ((c + 1) % 2) + i)
+
+        def base(c, a, stop):
+            for i in range(TILES):
+                k0 = c * WIDE + i * P
+                mx_pass(acc[c, i], w_q[a], slice(k0, k0 + P), dy_q[a], a == 0, stop)
+
+        def quantize_ad(c):
+            return quantize("ad%d" % c, interleave(ad_raw[:, :, c * WIDE : (c + 1) * WIDE], SCALAR_COLS_AD), E4M3)
+
+        def adapter(c, ad_q, stop):
+            for i in range(TILES):
+                mx_pass(acc[c, i], ad_q, slice(i * P, (i + 1) * P), h_q, False, stop)
 
         def finish(c):
-            ad_q = quantize("ad%d" % c, interleave(ad_raw[c]), E4M3)
-            for i in range(TILES):
-                mx_pass(acc[c, i], ad_q, slice(i * P, (i + 1) * P), h_q, False, True)
             for i in range(TILES):
                 nc.vector.tensor_tensor(out=sums[c][:, i, :], in0=acc[c, i][:], in1=sums[c][:, i, :], op=mybir.AluOpType.add)
             nc.sync.dma_start(
                 out=out_0[c * WIDE : (c + 1) * WIDE, :].rearrange("(i p) t -> p i t", p=P), in_=sums[c][:]
             )
 
-        base([0, 1])
+        open_banks(0)
+        open_banks(1)
+        for a in range(PASSES - 1):
+            base(0, a, False)
+            base(1, a, False)
+        for c in range(2):
+            adapter(c, quantize_ad(c), False)
+            base(c, PASSES - 1, True)
         finish(0)
-        base([2])
+        ad_last = quantize_ad(2)
         finish(1)
+        open_banks(2)
+        for a in range(PASSES):
+            base(2, a, False)
+        adapter(2, ad_last, True)
         finish(2)

@@ -80,28 +80,34 @@ def tile_mix_lrbwd_res_kernel(tc, dy, w8_words, w8_scales, bu, ad, res, out_0, o
         w_plane = keep.tile([P, PASSES * K], U8, name="w_plane", align_bytes=64)
         nc.vector.memset(w_plane[:].bitcast(I32), 0)
 
+        dy_raw = [load_rows("dy_raw%d" % a, dy[a * K_PASS : (a + 1) * K_PASS, :]) for a in range(PASSES)]
+        bu_raw = [load_rows("bu_raw%d" % a, bu[a * K_PASS : (a + 1) * K_PASS, :]) for a in range(PASSES)]
         for r in range(4):
-            nc.gpsimd.dma_start(
+            nc.sync.dma_start(
                 out=w_plane[r:P:32, :].bitcast(I32).rearrange("q (a n) -> q a n", a=PASSES),
                 in_=w8_scales[:, r:16:4, :].bitcast(I32).rearrange("a q n -> q a n"),
             )
-        dy_raw = [load_rows("dy_raw%d" % a, dy[a * K_PASS : (a + 1) * K_PASS, :]) for a in range(PASSES)]
-        bu_raw = [load_rows("bu_raw%d" % a, bu[a * K_PASS : (a + 1) * K_PASS, :]) for a in range(PASSES)]
-        w_q = []
-        for a in range(PASSES):
-            if a == PASSES - 1:
-                ad_raw = load_rows("ad_raw", ad)
+
+        def load_w(a):
             w_codes = keep.tile([P, K], U32, name="w_codes%d" % a, align_bytes=64)
             nc.sync.dma_start(
                 out=w_codes[:].bitcast(I32),
                 in_=w8_words[a].rearrange("p n i -> p (n i)").bitcast(I32),
             )
-            w_q.append((w_codes, w_plane[:, a * K : (a + 1) * K]))
-        sums = []
-        for c in range(CHUNKS):
+            return w_codes, w_plane[:, a * K : (a + 1) * K]
+
+        def load_res(c):
             res_sb = keep.tile([P, TILES, T], F32, name="res%d" % c)
             nc.sync.dma_start(out=res_sb[:], in_=res[c * WIDE : (c + 1) * WIDE, :].rearrange("(i p) t -> p i t", p=P))
-            sums.append(res_sb)
+            return res_sb
+
+        w_q = [load_w(0), load_w(1)]
+        ad_first = load_rows("ad_first", ad[:, :WIDE])
+        w_q.append(load_w(2))
+        sums = [load_res(0)]
+        ad_rest = load_rows("ad_rest", ad[:, WIDE:])
+        sums.extend([load_res(1), load_res(2)])
+        ad_raw = [ad_first[:], ad_rest[:, :, :WIDE], ad_rest[:, :, WIDE:]]
 
         dy_q = [quantize("dy%d" % a, interleave(dy_raw[a][:], SCALAR_COLS), E5M2) for a in range(PASSES)]
         h_acc = [bank(s) for s in range(PACK)]
@@ -130,7 +136,7 @@ def tile_mix_lrbwd_res_kernel(tc, dy, w8_words, w8_scales, bu, ad, res, out_0, o
                 mx_pass(acc[c, i], w_q[a], slice(k0, k0 + P), dy_q[a], a == 0, stop)
 
         def quantize_ad(c):
-            return quantize("ad%d" % c, interleave(ad_raw[:, :, c * WIDE : (c + 1) * WIDE], SCALAR_COLS_AD), E4M3)
+            return quantize("ad%d" % c, interleave(ad_raw[c], SCALAR_COLS_AD), E4M3)
 
         def adapter(c, ad_q, stop):
             for i in range(TILES):
@@ -145,17 +151,16 @@ def tile_mix_lrbwd_res_kernel(tc, dy, w8_words, w8_scales, bu, ad, res, out_0, o
 
         open_banks(0)
         open_banks(1)
-        for a in range(PASSES - 1):
+        for a in range(PASSES):
             base(0, a, False)
+            if a == PASSES - 1:
+                adapter(0, quantize_ad(0), True)
             base(1, a, False)
-        for c in range(2):
-            adapter(c, quantize_ad(c), False)
-            base(c, PASSES - 1, True)
         finish(0)
-        ad_last = quantize_ad(2)
-        finish(1)
         open_banks(2)
         for a in range(PASSES):
             base(2, a, False)
-        adapter(2, ad_last, True)
-        finish(2)
+        for c in range(1, CHUNKS):
+            adapter(c, quantize_ad(c), True)
+        for c in range(1, CHUNKS):
+            finish(c)

@@ -53,11 +53,11 @@ def tile_mix_lrbwd_res_kernel(tc, dy, w8_words, w8_scales, bu, ad, res, out_0, o
             nc.vector.tensor_copy(out=dst[:, cut:], in_=src[:, cut:])
             return grouped
 
-        def interleave_permuted(raw):
+        def interleave_permuted(raw, scalar_cols):
             grouped = stage.tile([P, WIDE * PACK], BF16, name="grouped", align_bytes=64)
             dst = grouped[:].rearrange("p (s m j) -> p m s j", s=PACK, j=PACK)
-            src = raw[:].rearrange("p j (m s) -> p m s j", s=PACK)
-            cut = SCALAR_COLS // 4
+            src = raw.rearrange("p j (m s) -> p m s j", s=PACK)
+            cut = scalar_cols // 4
             nc.scalar.copy(out=dst[:, :cut], in_=src[:, :cut])
             nc.vector.tensor_copy(out=dst[:, cut:], in_=src[:, cut:])
             return grouped
@@ -77,51 +77,72 @@ def tile_mix_lrbwd_res_kernel(tc, dy, w8_words, w8_scales, bu, ad, res, out_0, o
             acc = psum.tile([P, WIDE], F32, name="bank%d" % b)
             return acc
 
-        w_plane = keep.tile([P, PASSES * K], U8, name="w_plane", align_bytes=64)
-        nc.vector.memset(w_plane[:].bitcast(I32), 0)
+        plane_raw = keep.tile([P, PASSES * K], U8, name="plane_raw", align_bytes=64)
+        nc.vector.memset(plane_raw[:].bitcast(I32), 0)
 
-        dy_raw = [load_rows("dy_raw%d" % a, dy[a * K_PASS : (a + 1) * K_PASS, :]) for a in range(PASSES)]
-        bu_raw = [load_rows("bu_raw%d" % a, bu[a * K_PASS : (a + 1) * K_PASS, :]) for a in range(PASSES)]
+        dy_raw = [load_rows("dy_raw0", dy[:K_PASS, :])]
         for r in range(4):
             nc.sync.dma_start(
-                out=w_plane[r:P:32, :].bitcast(I32).rearrange("q (a n) -> q a n", a=PASSES),
+                out=plane_raw[r:P:32, :].bitcast(I32).rearrange("q (a n) -> q a n", a=PASSES),
                 in_=w8_scales[:, r:16:4, :].bitcast(I32).rearrange("a q n -> q a n"),
             )
+        dy_raw.extend([load_rows("dy_raw%d" % a, dy[a * K_PASS : (a + 1) * K_PASS, :]) for a in range(1, PASSES)])
+        bu_raw = [load_rows("bu_raw%d" % a, bu[a * K_PASS : (a + 1) * K_PASS, :]) for a in range(PASSES)]
 
         def load_w(a):
-            w_codes = keep.tile([P, K], U32, name="w_codes%d" % a, align_bytes=64)
-            nc.sync.dma_start(
-                out=w_codes[:].bitcast(I32),
-                in_=w8_words[a].rearrange("p n i -> p (n i)").bitcast(I32),
+            words = keep.tile([P, K], I32, name="w_raw%d" % a, align_bytes=64)
+            nc.sync.dma_start(out=words[:], in_=w8_words[a].rearrange("p n i -> p (n i)").bitcast(I32))
+            return words
+
+        def permute_scales(a):
+            plane = keep.tile([P, K], U8, name="w_scales%d" % a, align_bytes=64)
+            nc.vector.tensor_copy(
+                out=plane[:].rearrange("p (c s m) -> p s c m", c=CHUNKS, s=PACK),
+                in_=plane_raw[:, a * K : (a + 1) * K].rearrange("p (c m s) -> p s c m", c=CHUNKS, s=PACK),
             )
-            return w_codes, w_plane[:, a * K : (a + 1) * K]
+            return plane
+
+        def permute_words(a):
+            codes = keep.tile([P, K], U32, name="w_codes%d" % a, align_bytes=64)
+            nc.vector.tensor_copy(
+                out=codes[:].bitcast(I32).rearrange("p (c s g i) -> p g c s i", c=CHUNKS, s=PACK, i=4),
+                in_=w_raw[a][:].rearrange("p (c g i s) -> p g c s i", c=CHUNKS, s=PACK, i=4),
+            )
+            return codes, w_scales[a]
 
         def load_res(c):
             res_sb = keep.tile([P, TILES, T], F32, name="res%d" % c)
-            nc.sync.dma_start(out=res_sb[:], in_=res[c * WIDE : (c + 1) * WIDE, :].rearrange("(i p) t -> p i t", p=P))
+            nc.sync.dma_start(out=res_sb[:], in_=res[c * WIDE : (c + 1) * WIDE, :].rearrange("(p s) t -> p s t", s=PACK))
             return res_sb
 
-        w_q = [load_w(0), load_w(1)]
+        w_raw = [load_w(0), load_w(1)]
         ad_first = load_rows("ad_first", ad[:, :WIDE])
-        w_q.append(load_w(2))
+        w_raw.append(load_w(2))
         sums = [load_res(0)]
         ad_rest = load_rows("ad_rest", ad[:, WIDE:])
         sums.extend([load_res(1), load_res(2)])
         ad_raw = [ad_first[:], ad_rest[:, :, :WIDE], ad_rest[:, :, WIDE:]]
 
-        dy_q = [quantize("dy%d" % a, interleave(dy_raw[a][:], SCALAR_COLS), E5M2) for a in range(PASSES)]
+        dy_q = []
+        w_scales = []
+        for a in range(PASSES):
+            dy_q.append(quantize("dy%d" % a, interleave(dy_raw[a][:], SCALAR_COLS_AD), E5M2))
+            w_scales.append(permute_scales(a))
         h_acc = [bank(s) for s in range(PACK)]
         for a in range(PASSES):
-            bu_q = quantize("bu%d" % a, interleave_permuted(bu_raw[a]), E4M3)
+            bu_q = quantize("bu%d" % a, interleave_permuted(bu_raw[a][:], SCALAR_COLS), E4M3)
             for s in range(PACK):
                 mx_pass(h_acc[s], bu_q, slice(s * P, (s + 1) * P), dy_q[a], a == 0, a == PASSES - 1)
+        w_q = [permute_words(0)]
         h_sb = keep.tile([P, PACK, T], F32, name="h_sb")
         for s in range(PACK):
             if s % 2 == 0:
                 nc.scalar.copy(out=h_sb[:, s, :], in_=h_acc[s][:])
             else:
                 nc.vector.tensor_copy(out=h_sb[:, s, :], in_=h_acc[s][:])
-        h_q = quantize("h", interleave(h_sb[:], SCALAR_COLS), E5M2)
+        h_grouped = interleave(h_sb[:], SCALAR_COLS)
+        w_q.append(permute_words(1))
+        h_q = quantize("h", h_grouped, E5M2)
         nc.sync.dma_start(out=out_1.rearrange("(p j) t -> p j t", j=PACK), in_=h_sb[:])
 
         acc = {}
@@ -136,7 +157,7 @@ def tile_mix_lrbwd_res_kernel(tc, dy, w8_words, w8_scales, bu, ad, res, out_0, o
                 mx_pass(acc[c, i], w_q[a], slice(k0, k0 + P), dy_q[a], a == 0, stop)
 
         def quantize_ad(c):
-            return quantize("ad%d" % c, interleave(ad_raw[c], SCALAR_COLS_AD), E4M3)
+            return quantize("ad%d" % c, interleave_permuted(ad_raw[c], SCALAR_COLS_AD), E4M3)
 
         def adapter(c, ad_q, stop):
             for i in range(TILES):
@@ -146,16 +167,18 @@ def tile_mix_lrbwd_res_kernel(tc, dy, w8_words, w8_scales, bu, ad, res, out_0, o
             for i in range(TILES):
                 nc.vector.tensor_tensor(out=sums[c][:, i, :], in0=acc[c, i][:], in1=sums[c][:, i, :], op=mybir.AluOpType.add)
             nc.sync.dma_start(
-                out=out_0[c * WIDE : (c + 1) * WIDE, :].rearrange("(i p) t -> p i t", p=P), in_=sums[c][:]
+                out=out_0[c * WIDE : (c + 1) * WIDE, :].rearrange("(p s) t -> p s t", s=PACK), in_=sums[c][:]
             )
 
         open_banks(0)
         open_banks(1)
-        for a in range(PASSES):
+        for a in range(PASSES - 1):
             base(0, a, False)
-            if a == PASSES - 1:
-                adapter(0, quantize_ad(0), True)
             base(1, a, False)
+        adapter(0, quantize_ad(0), False)
+        w_q.append(permute_words(2))
+        base(0, PASSES - 1, True)
+        base(1, PASSES - 1, False)
         finish(0)
         open_banks(2)
         for a in range(PASSES):

@@ -21,7 +21,8 @@ WIDE = 512
 CHUNKS = K // WIDE
 TILES = WIDE // P
 SCALAR_COLS = 192
-SCALAR_COLS_AD = 256
+SCALAR_COLS_DY = 256
+SCALAR_COLS_AD = 320
 
 
 def tile_mix_lrbwd_res_kernel(tc, dy, w8_words, w8_scales, bu, ad, res, out_0, out_1):
@@ -34,7 +35,7 @@ def tile_mix_lrbwd_res_kernel(tc, dy, w8_words, w8_scales, bu, ad, res, out_0, o
         ctx.enter_context(tc.manual_schedule())
 
         def load_rows(name, rows):
-            raw = keep.tile([P, PACK, rows.shape[1]], F32, name=name)
+            raw = keep.tile([P, PACK, rows.shape[1]], F32, name=name, align_bytes=256)
             nc.sync.dma_start(out=raw[:], in_=rows.rearrange("(p j) w -> p j w", j=PACK))
             return raw
 
@@ -77,7 +78,7 @@ def tile_mix_lrbwd_res_kernel(tc, dy, w8_words, w8_scales, bu, ad, res, out_0, o
             acc = psum.tile([P, WIDE], F32, name="bank%d" % b)
             return acc
 
-        plane_raw = keep.tile([P, PASSES * K], U8, name="plane_raw", align_bytes=64)
+        plane_raw = keep.tile([P, PASSES * K], U8, name="plane_raw", align_bytes=256)
         nc.vector.memset(plane_raw[:].bitcast(I32), 0)
 
         dy_raw = [load_rows("dy_raw0", dy[:K_PASS, :])]
@@ -90,7 +91,7 @@ def tile_mix_lrbwd_res_kernel(tc, dy, w8_words, w8_scales, bu, ad, res, out_0, o
         bu_raw = [load_rows("bu_raw%d" % a, bu[a * K_PASS : (a + 1) * K_PASS, :]) for a in range(PASSES)]
 
         def load_w(a):
-            words = keep.tile([P, K], I32, name="w_raw%d" % a, align_bytes=64)
+            words = keep.tile([P, K], I32, name="w_raw%d" % a, align_bytes=256)
             nc.sync.dma_start(out=words[:], in_=w8_words[a].rearrange("p n i -> p (n i)").bitcast(I32))
             return words
 
@@ -108,42 +109,38 @@ def tile_mix_lrbwd_res_kernel(tc, dy, w8_words, w8_scales, bu, ad, res, out_0, o
                 out=codes[:].bitcast(I32).rearrange("p (c s g i) -> p g c s i", c=CHUNKS, s=PACK, i=4),
                 in_=w_raw[a][:].rearrange("p (c g i s) -> p g c s i", c=CHUNKS, s=PACK, i=4),
             )
-            return codes, w_scales[a]
+            return codes
 
         def load_res(c):
-            res_sb = keep.tile([P, TILES, T], F32, name="res%d" % c)
+            res_sb = keep.tile([P, TILES, T], F32, name="res%d" % c, align_bytes=256)
             nc.sync.dma_start(out=res_sb[:], in_=res[c * WIDE : (c + 1) * WIDE, :].rearrange("(p s) t -> p s t", s=PACK))
             return res_sb
 
-        w_raw = [load_w(0), load_w(1)]
-        ad_first = load_rows("ad_first", ad[:, :WIDE])
-        w_raw.append(load_w(2))
-        sums = [load_res(0)]
-        ad_rest = load_rows("ad_rest", ad[:, WIDE:])
-        sums.extend([load_res(1), load_res(2)])
-        ad_raw = [ad_first[:], ad_rest[:, :, :WIDE], ad_rest[:, :, WIDE:]]
+        w_raw = [load_w(a) for a in range(PASSES)]
+        ad_raw = load_rows("ad_raw", ad)
+        sums = [load_res(c) for c in range(CHUNKS)]
 
         dy_q = []
         w_scales = []
         for a in range(PASSES):
-            dy_q.append(quantize("dy%d" % a, interleave(dy_raw[a][:], SCALAR_COLS_AD), E5M2))
+            dy_q.append(quantize("dy%d" % a, interleave(dy_raw[a][:], SCALAR_COLS_DY), E5M2))
             w_scales.append(permute_scales(a))
         h_acc = [bank(s) for s in range(PACK)]
         for a in range(PASSES):
             bu_q = quantize("bu%d" % a, interleave_permuted(bu_raw[a][:], SCALAR_COLS), E4M3)
             for s in range(PACK):
                 mx_pass(h_acc[s], bu_q, slice(s * P, (s + 1) * P), dy_q[a], a == 0, a == PASSES - 1)
-        w_q = [permute_words(0)]
-        h_sb = keep.tile([P, PACK, T], F32, name="h_sb")
+        h_sb = keep.tile([P, PACK, T], F32, name="h_sb", align_bytes=256)
         for s in range(PACK):
             if s % 2 == 0:
                 nc.scalar.copy(out=h_sb[:, s, :], in_=h_acc[s][:])
             else:
                 nc.vector.tensor_copy(out=h_sb[:, s, :], in_=h_acc[s][:])
-        h_grouped = interleave(h_sb[:], SCALAR_COLS)
-        w_q.append(permute_words(1))
-        h_q = quantize("h", h_grouped, E5M2)
         nc.sync.dma_start(out=out_1.rearrange("(p j) t -> p j t", j=PACK), in_=h_sb[:])
+        h_grouped = interleave(h_sb[:], SCALAR_COLS)
+        w_q = [(permute_words(0), w_scales[0])]
+        h_q = quantize("h", h_grouped, E5M2)
+        w_q.extend([(permute_words(a), w_scales[a]) for a in range(1, PASSES)])
 
         acc = {}
 
@@ -151,39 +148,46 @@ def tile_mix_lrbwd_res_kernel(tc, dy, w8_words, w8_scales, bu, ad, res, out_0, o
             for i in range(TILES):
                 acc[c, i] = bank(TILES * ((c + 1) % 2) + i)
 
-        def base(c, a, stop):
-            for i in range(TILES):
-                k0 = c * WIDE + i * P
-                mx_pass(acc[c, i], w_q[a], slice(k0, k0 + P), dy_q[a], a == 0, stop)
+        def base(c, i, a):
+            k0 = c * WIDE + i * P
+            mx_pass(acc[c, i], w_q[a], slice(k0, k0 + P), dy_q[a], a == 0, False)
 
-        def quantize_ad(c):
-            return quantize("ad%d" % c, interleave_permuted(ad_raw[c], SCALAR_COLS_AD), E4M3)
+        def group_ad(c, scalar_cols):
+            return interleave_permuted(ad_raw[:, :, c * WIDE : (c + 1) * WIDE], scalar_cols)
 
-        def adapter(c, ad_q, stop):
-            for i in range(TILES):
-                mx_pass(acc[c, i], ad_q, slice(i * P, (i + 1) * P), h_q, False, stop)
+        def adapter(c, i):
+            mx_pass(acc[c, i], ad_q[c], slice(i * P, (i + 1) * P), h_q, False, True)
 
-        def finish(c):
-            for i in range(TILES):
-                nc.vector.tensor_tensor(out=sums[c][:, i, :], in0=acc[c, i][:], in1=sums[c][:, i, :], op=mybir.AluOpType.add)
+        def add_res(c, i):
+            nc.vector.tensor_tensor(out=sums[c][:, i, :], in0=acc[c, i][:], in1=sums[c][:, i, :], op=mybir.AluOpType.add)
+
+        def store(c):
             nc.sync.dma_start(
                 out=out_0[c * WIDE : (c + 1) * WIDE, :].rearrange("(p s) t -> p s t", s=PACK), in_=sums[c][:]
             )
 
-        open_banks(0)
-        open_banks(1)
-        for a in range(PASSES - 1):
-            base(0, a, False)
-            base(1, a, False)
-        adapter(0, quantize_ad(0), False)
-        w_q.append(permute_words(2))
-        base(0, PASSES - 1, True)
-        base(1, PASSES - 1, False)
-        finish(0)
-        open_banks(2)
+        for c in range(CHUNKS - 1):
+            open_banks(c)
         for a in range(PASSES):
-            base(2, a, False)
+            for c in range(CHUNKS - 1):
+                for i in range(TILES):
+                    base(c, i, a)
+        grouped = [group_ad(0, SCALAR_COLS), group_ad(1, SCALAR_COLS_AD)]
+        ad_q = [quantize("ad%d" % c, grouped[c], E4M3) for c in range(CHUNKS - 1)]
+        for c in range(CHUNKS - 1):
+            for i in range(TILES):
+                adapter(c, i)
+        last_grouped = group_ad(2, SCALAR_COLS_AD)
+        for i in range(TILES):
+            add_res(0, i)
+        store(0)
+        ad_q.append(quantize("ad2", last_grouped, E4M3))
+        open_banks(2)
+        for i in range(TILES):
+            for a in range(PASSES):
+                base(2, i, a)
+            adapter(2, i)
         for c in range(1, CHUNKS):
-            adapter(c, quantize_ad(c), True)
-        for c in range(1, CHUNKS):
-            finish(c)
+            for i in range(TILES):
+                add_res(c, i)
+            store(c)

@@ -21,8 +21,9 @@ WIDE = 512
 CHUNKS = K // WIDE
 TILES = WIDE // P
 SCALAR_COLS = 192
-SCALAR_COLS_DY = 256
-SCALAR_COLS_AD = 320
+SCALAR_COLS_DY = 352
+SCALAR_COLS_BU = 320
+SCALAR_COLS_AD = 256
 
 
 def tile_mix_lrbwd_res_kernel(tc, dy, w8_words, w8_scales, bu, ad, res, out_0, out_1):
@@ -60,7 +61,8 @@ def tile_mix_lrbwd_res_kernel(tc, dy, w8_words, w8_scales, bu, ad, res, out_0, o
             src = raw.rearrange("p j (m s) -> p m s j", s=PACK)
             cut = scalar_cols // 4
             nc.scalar.copy(out=dst[:, :cut], in_=src[:, :cut])
-            nc.vector.tensor_copy(out=dst[:, cut:], in_=src[:, cut:])
+            if scalar_cols < WIDE:
+                nc.vector.tensor_copy(out=dst[:, cut:], in_=src[:, cut:])
             return grouped
 
         def mx_pass(acc, lhs, cols, rhs, start, stop):
@@ -88,7 +90,6 @@ def tile_mix_lrbwd_res_kernel(tc, dy, w8_words, w8_scales, bu, ad, res, out_0, o
                 in_=w8_scales[:, r:16:4, :].bitcast(I32).rearrange("a q n -> q a n"),
             )
         dy_raw.extend([load_rows("dy_raw%d" % a, dy[a * K_PASS : (a + 1) * K_PASS, :]) for a in range(1, PASSES)])
-        bu_raw = [load_rows("bu_raw%d" % a, bu[a * K_PASS : (a + 1) * K_PASS, :]) for a in range(PASSES)]
 
         def load_w(a):
             words = keep.tile([P, K], I32, name="w_raw%d" % a, align_bytes=256)
@@ -103,21 +104,24 @@ def tile_mix_lrbwd_res_kernel(tc, dy, w8_words, w8_scales, bu, ad, res, out_0, o
             )
             return plane
 
-        def permute_words(a):
-            codes = keep.tile([P, K], U32, name="w_codes%d" % a, align_bytes=64)
+        w_codes = [keep.tile([P, K], U32, name="w_codes%d" % a, align_bytes=64) for a in range(PASSES)]
+
+        def permute_words(a, c0, c1):
+            cols = slice(c0 * WIDE, c1 * WIDE)
             nc.vector.tensor_copy(
-                out=codes[:].bitcast(I32).rearrange("p (c s g i) -> p g c s i", c=CHUNKS, s=PACK, i=4),
-                in_=w_raw[a][:].rearrange("p (c g i s) -> p g c s i", c=CHUNKS, s=PACK, i=4),
+                out=w_codes[a][:, cols].bitcast(I32).rearrange("p (c s g i) -> p g c s i", s=PACK, g=P // 4, i=4),
+                in_=w_raw[a][:, cols].rearrange("p (c g i s) -> p g c s i", s=PACK, g=P // 4, i=4),
             )
-            return codes
 
         def load_res(c):
             res_sb = keep.tile([P, TILES, T], F32, name="res%d" % c, align_bytes=256)
             nc.sync.dma_start(out=res_sb[:], in_=res[c * WIDE : (c + 1) * WIDE, :].rearrange("(p s) t -> p s t", s=PACK))
             return res_sb
 
-        w_raw = [load_w(a) for a in range(PASSES)]
+        w_raw = [load_w(a) for a in range(PASSES - 1)]
+        bu_raw = [load_rows("bu_raw%d" % a, bu[a * K_PASS : (a + 1) * K_PASS, :]) for a in range(PASSES)]
         ad_raw = load_rows("ad_raw", ad)
+        w_raw.append(load_w(PASSES - 1))
         sums = [load_res(c) for c in range(CHUNKS)]
 
         dy_q = []
@@ -125,9 +129,40 @@ def tile_mix_lrbwd_res_kernel(tc, dy, w8_words, w8_scales, bu, ad, res, out_0, o
         for a in range(PASSES):
             dy_q.append(quantize("dy%d" % a, interleave(dy_raw[a][:], SCALAR_COLS_DY), E5M2))
             w_scales.append(permute_scales(a))
+        acc = {}
+
+        def open_banks(c):
+            for i in range(TILES):
+                acc[c, i] = bank(TILES * ((c + 1) % 2) + i)
+
+        def base(c, i, a, stop):
+            k0 = c * WIDE + i * P
+            mx_pass(acc[c, i], w_q[a], slice(k0, k0 + P), dy_q[a], a == 0, stop)
+
+        def group_ad(c, scalar_cols):
+            return interleave_permuted(ad_raw[:, :, c * WIDE : (c + 1) * WIDE], scalar_cols)
+
+        def adapter(c, i, stop):
+            mx_pass(acc[c, i], ad_q[c], slice(i * P, (i + 1) * P), h_q, False, stop)
+
+        def add_res(c, i):
+            nc.vector.tensor_tensor(out=sums[c][:, i, :], in0=acc[c, i][:], in1=sums[c][:, i, :], op=mybir.AluOpType.add)
+
+        def store(c, i0, i1):
+            rows = out_0[c * WIDE : (c + 1) * WIDE, :].rearrange("(p s) t -> p s t", s=PACK)
+            nc.sync.dma_start(out=rows[:, i0:i1, :], in_=sums[c][:, i0:i1, :])
+
+        last = CHUNKS - 1
+        w_q = [(w_codes[a], w_scales[a]) for a in range(PASSES)]
+        open_banks(0)
+        for a in range(PASSES - 1):
+            permute_words(a, 0, CHUNKS)
+            for i in range(TILES):
+                base(0, i, a, False)
+
         h_acc = [bank(s) for s in range(PACK)]
         for a in range(PASSES):
-            bu_q = quantize("bu%d" % a, interleave_permuted(bu_raw[a][:], SCALAR_COLS), E4M3)
+            bu_q = quantize("bu%d" % a, interleave_permuted(bu_raw[a][:], SCALAR_COLS if a == PASSES - 1 else SCALAR_COLS_BU), E4M3)
             for s in range(PACK):
                 mx_pass(h_acc[s], bu_q, slice(s * P, (s + 1) * P), dy_q[a], a == 0, a == PASSES - 1)
         h_sb = keep.tile([P, PACK, T], F32, name="h_sb", align_bytes=256)
@@ -137,57 +172,38 @@ def tile_mix_lrbwd_res_kernel(tc, dy, w8_words, w8_scales, bu, ad, res, out_0, o
             else:
                 nc.vector.tensor_copy(out=h_sb[:, s, :], in_=h_acc[s][:])
         nc.sync.dma_start(out=out_1.rearrange("(p j) t -> p j t", j=PACK), in_=h_sb[:])
-        h_grouped = interleave(h_sb[:], SCALAR_COLS)
-        w_q = [(permute_words(0), w_scales[0])]
-        h_q = quantize("h", h_grouped, E5M2)
-        w_q.extend([(permute_words(a), w_scales[a]) for a in range(1, PASSES)])
+        h_q = quantize("h", interleave(h_sb[:], SCALAR_COLS), E5M2)
 
-        acc = {}
-
-        def open_banks(c):
+        open_banks(1)
+        for a in range(PASSES - 1):
             for i in range(TILES):
-                acc[c, i] = bank(TILES * ((c + 1) % 2) + i)
-
-        def base(c, i, a):
-            k0 = c * WIDE + i * P
-            mx_pass(acc[c, i], w_q[a], slice(k0, k0 + P), dy_q[a], a == 0, False)
-
-        def group_ad(c, scalar_cols):
-            return interleave_permuted(ad_raw[:, :, c * WIDE : (c + 1) * WIDE], scalar_cols)
-
-        def adapter(c, i):
-            mx_pass(acc[c, i], ad_q[c], slice(i * P, (i + 1) * P), h_q, False, True)
-
-        def add_res(c, i):
-            nc.vector.tensor_tensor(out=sums[c][:, i, :], in0=acc[c, i][:], in1=sums[c][:, i, :], op=mybir.AluOpType.add)
-
-        def store(c):
-            nc.sync.dma_start(
-                out=out_0[c * WIDE : (c + 1) * WIDE, :].rearrange("(p s) t -> p s t", s=PACK), in_=sums[c][:]
-            )
-
-        for c in range(CHUNKS - 1):
-            open_banks(c)
-        for a in range(PASSES):
-            for c in range(CHUNKS - 1):
-                for i in range(TILES):
-                    base(c, i, a)
-        grouped = [group_ad(0, SCALAR_COLS), group_ad(1, SCALAR_COLS_AD)]
-        ad_q = [quantize("ad%d" % c, grouped[c], E4M3) for c in range(CHUNKS - 1)]
-        for c in range(CHUNKS - 1):
-            for i in range(TILES):
-                adapter(c, i)
-        last_grouped = group_ad(2, SCALAR_COLS_AD)
+                base(1, i, a, False)
+        ad_q = [quantize("ad0", group_ad(0, SCALAR_COLS), E4M3)]
+        permute_words(PASSES - 1, 0, 1)
+        grouped = [group_ad(1, SCALAR_COLS_AD), group_ad(last, WIDE)]
+        permute_words(PASSES - 1, 1, CHUNKS)
+        ad_q.append(quantize("ad1", grouped[0], E4M3))
+        for i in range(TILES):
+            adapter(0, i, False)
+        for i in range(TILES):
+            base(0, i, PASSES - 1, True)
+        for i in range(TILES):
+            base(1, i, PASSES - 1, False)
+        for i in range(TILES):
+            adapter(1, i, True)
         for i in range(TILES):
             add_res(0, i)
-        store(0)
-        ad_q.append(quantize("ad2", last_grouped, E4M3))
-        open_banks(2)
+        store(0, 0, TILES)
+        ad_q.append(quantize("ad2", grouped[1], E4M3))
+        open_banks(last)
         for i in range(TILES):
             for a in range(PASSES):
-                base(2, i, a)
-            adapter(2, i)
-        for c in range(1, CHUNKS):
-            for i in range(TILES):
-                add_res(c, i)
-            store(c)
+                base(last, i, a, False)
+            adapter(last, i, True)
+        for i in range(TILES):
+            add_res(1, i)
+        store(1, 0, TILES)
+        for i0 in range(0, TILES, 2):
+            add_res(last, i0)
+            add_res(last, i0 + 1)
+            store(last, i0, i0 + 2)

@@ -23,7 +23,7 @@ TILES = WIDE // P
 SCALAR_COLS = 192
 SCALAR_COLS_DY = 352
 SCALAR_COLS_BU = 320
-SCALAR_COLS_AD = 256
+SCALAR_COLS_AD = 320
 
 
 def tile_mix_lrbwd_res_kernel(tc, dy, w8_words, w8_scales, bu, ad, res, out_0, out_1):
@@ -154,11 +154,8 @@ def tile_mix_lrbwd_res_kernel(tc, dy, w8_words, w8_scales, bu, ad, res, out_0, o
 
         last = CHUNKS - 1
         w_q = [(w_codes[a], w_scales[a]) for a in range(PASSES)]
-        open_banks(0)
         for a in range(PASSES - 1):
             permute_words(a, 0, CHUNKS)
-            for i in range(TILES):
-                base(0, i, a, False)
 
         h_acc = [bank(s) for s in range(PACK)]
         for a in range(PASSES):
@@ -174,10 +171,11 @@ def tile_mix_lrbwd_res_kernel(tc, dy, w8_words, w8_scales, bu, ad, res, out_0, o
         nc.sync.dma_start(out=out_1.rearrange("(p j) t -> p j t", j=PACK), in_=h_sb[:])
         h_q = quantize("h", interleave(h_sb[:], SCALAR_COLS), E5M2)
 
-        open_banks(1)
-        for a in range(PASSES - 1):
-            for i in range(TILES):
-                base(1, i, a, False)
+        for c in range(last):
+            open_banks(c)
+            for a in range(PASSES - 1):
+                for i in range(TILES):
+                    base(c, i, a, False)
         ad_q = [quantize("ad0", group_ad(0, SCALAR_COLS), E4M3)]
         permute_words(PASSES - 1, 0, 1)
         grouped = [group_ad(1, SCALAR_COLS_AD), group_ad(last, WIDE)]

@@ -21,9 +21,9 @@ WIDE = 512
 CHUNKS = K // WIDE
 TILES = WIDE // P
 SCALAR_COLS = 192
-SCALAR_COLS_DY = 352
-SCALAR_COLS_BU = 320
-SCALAR_COLS_AD = 320
+SCALAR_COLS_HALF = 256
+SCALAR_COLS_DY = 320
+SCALAR_COLS_AD = 384
 
 
 def tile_mix_lrbwd_res_kernel(tc, dy, w8_words, w8_scales, bu, ad, res, out_0, out_1):
@@ -41,9 +41,9 @@ def tile_mix_lrbwd_res_kernel(tc, dy, w8_words, w8_scales, bu, ad, res, out_0, o
             return raw
 
         def quantize(name, grouped, fmt):
-            codes = keep.tile([P, WIDE], U32, name=name + "_codes", align_bytes=64)
-            scales = keep.tile([P, WIDE], U8, name=name + "_scales", align_bytes=64)
-            nc.vector.quantize_mx(out=codes[:].bitcast(fmt), scales=scales[:], in_=grouped[:])
+            codes = keep.tile([P, grouped.shape[1] // PACK], U32, name=name + "_codes", align_bytes=64)
+            scales = keep.tile([P, grouped.shape[1] // PACK], U8, name=name + "_scales", align_bytes=64)
+            nc.vector.quantize_mx(out=codes[:].bitcast(fmt), scales=scales[:], in_=grouped)
             return codes, scales
 
         def interleave(raw, scalar_cols):
@@ -53,7 +53,7 @@ def tile_mix_lrbwd_res_kernel(tc, dy, w8_words, w8_scales, bu, ad, res, out_0, o
             cut = scalar_cols // 4
             nc.scalar.copy(out=dst[:, :cut], in_=src[:, :cut])
             nc.vector.tensor_copy(out=dst[:, cut:], in_=src[:, cut:])
-            return grouped
+            return grouped[:]
 
         def interleave_permuted(raw, scalar_cols):
             grouped = stage.tile([P, WIDE * PACK], BF16, name="grouped", align_bytes=64)
@@ -63,13 +63,29 @@ def tile_mix_lrbwd_res_kernel(tc, dy, w8_words, w8_scales, bu, ad, res, out_0, o
             nc.scalar.copy(out=dst[:, :cut], in_=src[:, :cut])
             if scalar_cols < WIDE:
                 nc.vector.tensor_copy(out=dst[:, cut:], in_=src[:, cut:])
-            return grouped
+            return grouped[:]
 
-        def mx_pass(acc, lhs, cols, rhs, start, stop):
+        def stationary_tiles(quantized):
+            codes, scales = quantized
+            return [(codes[:, m0 : m0 + P], scales[:, m0 : m0 + P]) for m0 in range(0, codes.shape[1], P)]
+
+        def quantize_in_halves(name, raw):
+            src = raw.rearrange("p j (m u s) -> p u m s j", u=2, s=2)
+            halves = []
+            for u, copy in enumerate((nc.vector.tensor_copy, nc.scalar.copy)):
+                half = keep.tile([P, WIDE * PACK // 2], BF16, name="%s_half%d" % (name, u), align_bytes=64)
+                copy(out=half[:].rearrange("p (s m j) -> p m s j", s=2, j=PACK), in_=src[:, u])
+                halves.append(half[:])
+            tiles = []
+            for u, half in enumerate(halves):
+                tiles.extend(stationary_tiles(quantize("%s_%d" % (name, u), half, E4M3)))
+            return tiles
+
+        def mx_pass(acc, codes, scales, rhs, start, stop):
             nc.tensor.matmul_mx(
                 out=acc[:],
-                lhsT=lhs[0][:, cols].bitcast(E4M3),
-                lhsT_scale=lhs[1][:, cols],
+                lhsT=codes.bitcast(E4M3),
+                lhsT_scale=scales,
                 rhs=rhs[0][:].bitcast(E5M2),
                 rhs_scale=rhs[1][:],
                 start=start,
@@ -83,17 +99,21 @@ def tile_mix_lrbwd_res_kernel(tc, dy, w8_words, w8_scales, bu, ad, res, out_0, o
         plane_raw = keep.tile([P, PASSES * K], U8, name="plane_raw", align_bytes=256)
         nc.vector.memset(plane_raw[:].bitcast(I32), 0)
 
-        dy_raw = [load_rows("dy_raw0", dy[:K_PASS, :])]
+        def load_passes(name, rows):
+            raw = keep.tile([P, PASSES, PACK * rows.shape[1]], F32, name=name, align_bytes=256)
+            nc.sync.dma_start(out=raw[:], in_=rows.rearrange("(a p j) w -> p a (j w)", a=PASSES, j=PACK))
+            return [raw[:, a, :].rearrange("p (j w) -> p j w", j=PACK) for a in range(PASSES)]
+
+        dy_raw = load_passes("dy_raw", dy)
         for r in range(4):
             nc.sync.dma_start(
                 out=plane_raw[r:P:32, :].bitcast(I32).rearrange("q (a n) -> q a n", a=PASSES),
                 in_=w8_scales[:, r:16:4, :].bitcast(I32).rearrange("a q n -> q a n"),
             )
-        dy_raw.extend([load_rows("dy_raw%d" % a, dy[a * K_PASS : (a + 1) * K_PASS, :]) for a in range(1, PASSES)])
 
-        def load_w(a):
-            words = keep.tile([P, K], I32, name="w_raw%d" % a, align_bytes=256)
-            nc.sync.dma_start(out=words[:], in_=w8_words[a].rearrange("p n i -> p (n i)").bitcast(I32))
+        def load_w():
+            words = keep.tile([P, PASSES, K], I32, name="w_raw", align_bytes=256)
+            nc.sync.dma_start(out=words[:], in_=w8_words.rearrange("a p n i -> p a (n i)").bitcast(I32))
             return words
 
         def permute_scales(a):
@@ -104,46 +124,47 @@ def tile_mix_lrbwd_res_kernel(tc, dy, w8_words, w8_scales, bu, ad, res, out_0, o
             )
             return plane
 
-        w_codes = [keep.tile([P, K], U32, name="w_codes%d" % a, align_bytes=64) for a in range(PASSES)]
-
-        def permute_words(a, c0, c1):
-            cols = slice(c0 * WIDE, c1 * WIDE)
+        def permute_words(c):
+            codes = keep.tile([P, PASSES * WIDE], U32, name="w_codes%d" % c, align_bytes=64)
             nc.vector.tensor_copy(
-                out=w_codes[a][:, cols].bitcast(I32).rearrange("p (c s g i) -> p g c s i", s=PACK, g=P // 4, i=4),
-                in_=w_raw[a][:, cols].rearrange("p (c g i s) -> p g c s i", s=PACK, g=P // 4, i=4),
+                out=codes[:].bitcast(I32).rearrange("p (a s g i) -> p g a s i", a=PASSES, s=PACK, i=4),
+                in_=w_raw[:, :, c * WIDE : (c + 1) * WIDE].rearrange("p a (g i s) -> p g a s i", s=PACK, i=4),
             )
+            return codes
 
         def load_res(c):
             res_sb = keep.tile([P, TILES, T], F32, name="res%d" % c, align_bytes=256)
             nc.sync.dma_start(out=res_sb[:], in_=res[c * WIDE : (c + 1) * WIDE, :].rearrange("(p s) t -> p s t", s=PACK))
             return res_sb
 
-        w_raw = [load_w(a) for a in range(PASSES - 1)]
-        bu_raw = [load_rows("bu_raw%d" % a, bu[a * K_PASS : (a + 1) * K_PASS, :]) for a in range(PASSES)]
+        bu_raw = load_passes("bu_raw", bu)
+        w_raw = load_w()
         ad_raw = load_rows("ad_raw", ad)
-        w_raw.append(load_w(PASSES - 1))
         sums = [load_res(c) for c in range(CHUNKS)]
 
         dy_q = []
         w_scales = []
+        ahead = interleave(dy_raw[0], SCALAR_COLS_DY)
         for a in range(PASSES):
-            dy_q.append(quantize("dy%d" % a, interleave(dy_raw[a][:], SCALAR_COLS_DY), E5M2))
+            ready = ahead
+            if a + 1 < PASSES:
+                ahead = interleave(dy_raw[a + 1], SCALAR_COLS_DY)
+            dy_q.append(quantize("dy%d" % a, ready, E5M2))
             w_scales.append(permute_scales(a))
         acc = {}
 
-        def open_banks(c):
-            for i in range(TILES):
-                acc[c, i] = bank(TILES * ((c + 1) % 2) + i)
-
-        def base(c, i, a, stop):
-            k0 = c * WIDE + i * P
-            mx_pass(acc[c, i], w_q[a], slice(k0, k0 + P), dy_q[a], a == 0, stop)
+        def base(c, i):
+            acc[c, i] = bank(TILES * ((c + 1) % 2) + i)
+            for a in range(PASSES):
+                w0 = a * WIDE + i * P
+                k0 = c * WIDE + i * P
+                mx_pass(acc[c, i], w_codes[c][:, w0 : w0 + P], w_scales[a][:, k0 : k0 + P], dy_q[a], a == 0, False)
 
         def group_ad(c, scalar_cols):
             return interleave_permuted(ad_raw[:, :, c * WIDE : (c + 1) * WIDE], scalar_cols)
 
-        def adapter(c, i, stop):
-            mx_pass(acc[c, i], ad_q[c], slice(i * P, (i + 1) * P), h_q, False, stop)
+        def adapter(c, i):
+            mx_pass(acc[c, i], ad_q[c][i][0], ad_q[c][i][1], h_q, False, True)
 
         def add_res(c, i):
             nc.vector.tensor_tensor(out=sums[c][:, i, :], in0=acc[c, i][:], in1=sums[c][:, i, :], op=mybir.AluOpType.add)
@@ -153,54 +174,54 @@ def tile_mix_lrbwd_res_kernel(tc, dy, w8_words, w8_scales, bu, ad, res, out_0, o
             nc.sync.dma_start(out=rows[:, i0:i1, :], in_=sums[c][:, i0:i1, :])
 
         last = CHUNKS - 1
-        w_q = [(w_codes[a], w_scales[a]) for a in range(PASSES)]
-        for a in range(PASSES - 1):
-            permute_words(a, 0, CHUNKS)
 
         h_acc = [bank(s) for s in range(PACK)]
         for a in range(PASSES):
-            bu_q = quantize("bu%d" % a, interleave_permuted(bu_raw[a][:], SCALAR_COLS if a == PASSES - 1 else SCALAR_COLS_BU), E4M3)
+            if a == 0:
+                bu_q = quantize_in_halves("bu0", bu_raw[0])
+            else:
+                bu_q = stationary_tiles(quantize("bu%d" % a, interleave_permuted(bu_raw[a], SCALAR_COLS_HALF), E4M3))
             for s in range(PACK):
-                mx_pass(h_acc[s], bu_q, slice(s * P, (s + 1) * P), dy_q[a], a == 0, a == PASSES - 1)
+                mx_pass(h_acc[s], bu_q[s][0], bu_q[s][1], dy_q[a], a == 0, a == PASSES - 1)
+        w_codes = [permute_words(0)]
         h_sb = keep.tile([P, PACK, T], F32, name="h_sb", align_bytes=256)
         for s in range(PACK):
-            if s % 2 == 0:
+            if s < PACK - 1:
                 nc.scalar.copy(out=h_sb[:, s, :], in_=h_acc[s][:])
             else:
                 nc.vector.tensor_copy(out=h_sb[:, s, :], in_=h_acc[s][:])
         nc.sync.dma_start(out=out_1.rearrange("(p j) t -> p j t", j=PACK), in_=h_sb[:])
+        w_codes.append(permute_words(1))
         h_q = quantize("h", interleave(h_sb[:], SCALAR_COLS), E5M2)
+        w_codes.append(permute_words(last))
 
         for c in range(last):
-            open_banks(c)
-            for a in range(PASSES - 1):
-                for i in range(TILES):
-                    base(c, i, a, False)
-        ad_q = [quantize("ad0", group_ad(0, SCALAR_COLS), E4M3)]
-        permute_words(PASSES - 1, 0, 1)
+            for i in range(TILES):
+                base(c, i)
+        ad_q = [quantize_in_halves("ad0", ad_raw[:, :, :WIDE])]
         grouped = [group_ad(1, SCALAR_COLS_AD), group_ad(last, WIDE)]
-        permute_words(PASSES - 1, 1, CHUNKS)
-        ad_q.append(quantize("ad1", grouped[0], E4M3))
         for i in range(TILES):
-            adapter(0, i, False)
-        for i in range(TILES):
-            base(0, i, PASSES - 1, True)
-        for i in range(TILES):
-            base(1, i, PASSES - 1, False)
-        for i in range(TILES):
-            adapter(1, i, True)
-        for i in range(TILES):
+            adapter(0, i)
+        for i in range(TILES - 1):
             add_res(0, i)
+        for i in range(TILES // 2):
+            base(last, i)
+        ad_q.append(stationary_tiles(quantize("ad1", grouped[0], E4M3)))
+        for i in range(TILES):
+            adapter(1, i)
+        add_res(0, TILES - 1)
+        for i in range(TILES // 2, TILES):
+            base(last, i)
         store(0, 0, TILES)
-        ad_q.append(quantize("ad2", grouped[1], E4M3))
-        open_banks(last)
-        for i in range(TILES):
-            for a in range(PASSES):
-                base(last, i, a, False)
-            adapter(last, i, True)
-        for i in range(TILES):
+        for i in range(TILES - 1):
             add_res(1, i)
+        half = WIDE * PACK // 2
+        ad_q.append(stationary_tiles(quantize("ad2_0", grouped[1][:, :half], E4M3)))
+        add_res(1, TILES - 1)
         store(1, 0, TILES)
+        ad_q[last].extend(stationary_tiles(quantize("ad2_1", grouped[1][:, half:], E4M3)))
+        for i in range(TILES):
+            adapter(last, i)
         for i0 in range(0, TILES, 2):
             add_res(last, i0)
             add_res(last, i0 + 1)

@@ -101,7 +101,8 @@ def tile_mix_lrbwd_res_kernel(tc, dy, w8_words, w8_scales, bu, ad, res, out_0, o
 
         def load_passes(name, rows):
             raw = keep.tile([P, PASSES, PACK * rows.shape[1]], F32, name=name, align_bytes=256)
-            nc.sync.dma_start(out=raw[:], in_=rows.rearrange("(a p j) w -> p a (j w)", a=PASSES, j=PACK))
+            for a in range(PASSES):
+                nc.sync.dma_start(out=raw[:, a, :], in_=rows.rearrange("(a p j) w -> a p (j w)", a=PASSES, j=PACK)[a])
             return [raw[:, a, :].rearrange("p (j w) -> p j w", j=PACK) for a in range(PASSES)]
 
         dy_raw = load_passes("dy_raw", dy)
@@ -113,7 +114,8 @@ def tile_mix_lrbwd_res_kernel(tc, dy, w8_words, w8_scales, bu, ad, res, out_0, o
 
         def load_w():
             words = keep.tile([P, PASSES, K], I32, name="w_raw", align_bytes=256)
-            nc.sync.dma_start(out=words[:], in_=w8_words.rearrange("a p n i -> p a (n i)").bitcast(I32))
+            for a in range(PASSES):
+                nc.sync.dma_start(out=words[:, a, :], in_=w8_words[a].rearrange("p n i -> p (n i)").bitcast(I32))
             return words
 
         def permute_scales(a):

@@ -100,17 +100,16 @@ def tile_mix_lrbwd_res_kernel(tc, dy, w8_words, w8_scales, bu, ad, res, out_0, o
         nc.vector.memset(plane_raw[:].bitcast(I32), 0)
 
         def load_passes(name, rows):
-            raw = keep.tile([P, PASSES, PACK * rows.shape[1]], F32, name=name, align_bytes=256)
-            for a in range(PASSES):
-                nc.sync.dma_start(out=raw[:, a, :], in_=rows.rearrange("(a p j) w -> a p (j w)", a=PASSES, j=PACK)[a])
-            return [raw[:, a, :].rearrange("p (j w) -> p j w", j=PACK) for a in range(PASSES)]
+            return [load_rows("%s%d" % (name, a), rows[a * K_PASS : (a + 1) * K_PASS, :])[:] for a in range(PASSES)]
+
+        def load_scales(queue):
+            for r in range(4):
+                queue.dma_start(
+                    out=plane_raw[r:P:32, :].bitcast(I32).rearrange("q (a n) -> q a n", a=PASSES),
+                    in_=w8_scales[:, r:16:4, :].bitcast(I32).rearrange("a q n -> q a n"),
+                )
 
         dy_raw = load_passes("dy_raw", dy)
-        for r in range(4):
-            nc.sync.dma_start(
-                out=plane_raw[r:P:32, :].bitcast(I32).rearrange("q (a n) -> q a n", a=PASSES),
-                in_=w8_scales[:, r:16:4, :].bitcast(I32).rearrange("a q n -> q a n"),
-            )
 
         def load_w():
             words = keep.tile([P, PASSES, K], I32, name="w_raw", align_bytes=256)
@@ -118,11 +117,11 @@ def tile_mix_lrbwd_res_kernel(tc, dy, w8_words, w8_scales, bu, ad, res, out_0, o
                 nc.sync.dma_start(out=words[:, a, :], in_=w8_words[a].rearrange("p n i -> p (n i)").bitcast(I32))
             return words
 
-        def permute_scales(a):
-            plane = keep.tile([P, K], U8, name="w_scales%d" % a, align_bytes=64)
+        def permute_scales(c):
+            plane = keep.tile([P, PASSES * WIDE], U8, name="w_scales%d" % c, align_bytes=64)
             nc.vector.tensor_copy(
-                out=plane[:].rearrange("p (c s m) -> p s c m", c=CHUNKS, s=PACK),
-                in_=plane_raw[:, a * K : (a + 1) * K].rearrange("p (c m s) -> p s c m", c=CHUNKS, s=PACK),
+                out=plane[:].rearrange("p (a s m) -> p s a m", a=PASSES, s=PACK),
+                in_=plane_raw[:].rearrange("p (a c m s) -> p c s a m", a=PASSES, c=CHUNKS, s=PACK)[:, c],
             )
             return plane
 
@@ -141,26 +140,17 @@ def tile_mix_lrbwd_res_kernel(tc, dy, w8_words, w8_scales, bu, ad, res, out_0, o
 
         bu_raw = load_passes("bu_raw", bu)
         w_raw = load_w()
-        ad_raw = load_rows("ad_raw", ad)
-        sums = [load_res(c) for c in range(CHUNKS)]
 
         dy_q = []
-        w_scales = []
-        ahead = interleave(dy_raw[0], SCALAR_COLS_DY)
         for a in range(PASSES):
-            ready = ahead
-            if a + 1 < PASSES:
-                ahead = interleave(dy_raw[a + 1], SCALAR_COLS_DY)
-            dy_q.append(quantize("dy%d" % a, ready, E5M2))
-            w_scales.append(permute_scales(a))
+            dy_q.append(quantize("dy%d" % a, interleave(dy_raw[a], SCALAR_COLS_DY), E5M2))
         acc = {}
 
         def base(c, i):
             acc[c, i] = bank(TILES * ((c + 1) % 2) + i)
             for a in range(PASSES):
                 w0 = a * WIDE + i * P
-                k0 = c * WIDE + i * P
-                mx_pass(acc[c, i], w_codes[c][:, w0 : w0 + P], w_scales[a][:, k0 : k0 + P], dy_q[a], a == 0, False)
+                mx_pass(acc[c, i], w_codes[c][:, w0 : w0 + P], w_scales[c][:, w0 : w0 + P], dy_q[a], a == 0, False)
 
         def group_ad(c, scalar_cols):
             return interleave_permuted(ad_raw[:, :, c * WIDE : (c + 1) * WIDE], scalar_cols)
@@ -179,23 +169,29 @@ def tile_mix_lrbwd_res_kernel(tc, dy, w8_words, w8_scales, bu, ad, res, out_0, o
 
         h_acc = [bank(s) for s in range(PACK)]
         for a in range(PASSES):
-            if a == 0:
-                bu_q = quantize_in_halves("bu0", bu_raw[0])
+            if a == PASSES - 1:
+                bu_q = quantize_in_halves("bu%d" % a, bu_raw[a])
             else:
-                bu_q = stationary_tiles(quantize("bu%d" % a, interleave_permuted(bu_raw[a], SCALAR_COLS_HALF), E4M3))
+                bu_q = stationary_tiles(quantize("bu%d" % a, interleave_permuted(bu_raw[a], SCALAR_COLS), E4M3))
             for s in range(PACK):
                 mx_pass(h_acc[s], bu_q[s][0], bu_q[s][1], dy_q[a], a == 0, a == PASSES - 1)
-        w_codes = [permute_words(0)]
         h_sb = keep.tile([P, PACK, T], F32, name="h_sb", align_bytes=256)
         for s in range(PACK):
-            if s < PACK - 1:
+            if s % 2 == 1:
                 nc.scalar.copy(out=h_sb[:, s, :], in_=h_acc[s][:])
             else:
                 nc.vector.tensor_copy(out=h_sb[:, s, :], in_=h_acc[s][:])
-        nc.sync.dma_start(out=out_1.rearrange("(p j) t -> p j t", j=PACK), in_=h_sb[:])
+        nc.sync.dma_start(out=out_1.rearrange("(p j) t -> p j t", j=PACK), in_=h_sb[:], max_dma_last_dim=4096)
+        load_scales(nc.scalar)
+        ad_raw = load_rows("ad_raw", ad)
+        sums = [load_res(c) for c in range(CHUNKS)]
+        h_grouped = interleave(h_sb[:], SCALAR_COLS_HALF)
+        w_codes = [permute_words(0)]
+        h_q = quantize("h", h_grouped, E5M2)
         w_codes.append(permute_words(1))
-        h_q = quantize("h", interleave(h_sb[:], SCALAR_COLS), E5M2)
+        w_scales = [permute_scales(0), permute_scales(1)]
         w_codes.append(permute_words(last))
+        w_scales.append(permute_scales(last))
 
         for c in range(last):
             for i in range(TILES):

@@ -57,8 +57,8 @@ def tile_mix_lrbwd_res_kernel(tc, dy, w8_words, w8_scales, bu, ad, res, out_0, o
 
         def interleave_permuted(raw, scalar_cols):
             grouped = stage.tile([P, WIDE * PACK], BF16, name="grouped", align_bytes=64)
-            dst = grouped[:].rearrange("p (s m j) -> p m s j", s=PACK, j=PACK)
-            src = raw.rearrange("p j (m s) -> p m s j", s=PACK)
+            dst = grouped[:].rearrange("p (s m j) -> p m j s", s=PACK, j=PACK)
+            src = raw.rearrange("p j (m s) -> p m j s", s=PACK)
             cut = scalar_cols // 4
             nc.scalar.copy(out=dst[:, :cut], in_=src[:, :cut])
             if scalar_cols < WIDE:
@@ -70,11 +70,11 @@ def tile_mix_lrbwd_res_kernel(tc, dy, w8_words, w8_scales, bu, ad, res, out_0, o
             return [(codes[:, m0 : m0 + P], scales[:, m0 : m0 + P]) for m0 in range(0, codes.shape[1], P)]
 
         def quantize_in_halves(name, raw):
-            src = raw.rearrange("p j (m u s) -> p u m s j", u=2, s=2)
+            src = raw.rearrange("p j (m u s) -> p u m j s", u=2, s=2)
             halves = []
             for u, copy in enumerate((nc.vector.tensor_copy, nc.scalar.copy)):
                 half = keep.tile([P, WIDE * PACK // 2], BF16, name="%s_half%d" % (name, u), align_bytes=64)
-                copy(out=half[:].rearrange("p (s m j) -> p m s j", s=2, j=PACK), in_=src[:, u])
+                copy(out=half[:].rearrange("p (s m j) -> p m j s", s=2, j=PACK), in_=src[:, u])
                 halves.append(half[:])
             tiles = []
             for u, half in enumerate(halves):

@@ -111,27 +111,31 @@ def tile_mix_lrbwd_res_kernel(tc, dy, w8_words, w8_scales, bu, ad, res, out_0, o
 
         dy_raw = load_passes("dy_raw", dy)
 
-        def load_w():
-            words = keep.tile([P, PASSES, K], I32, name="w_raw", align_bytes=256)
-            for a in range(PASSES):
-                nc.sync.dma_start(out=words[:, a, :], in_=w8_words[a].rearrange("p n i -> p (n i)").bitcast(I32))
+        def load_w(a):
+            words = keep.tile([P, K], I32, name="w_raw%d" % a, align_bytes=256)
+            nc.sync.dma_start(out=words[:], in_=w8_words[a].rearrange("p n i -> p (n i)").bitcast(I32))
             return words
 
-        def permute_scales(c):
-            plane = keep.tile([P, PASSES * WIDE], U8, name="w_scales%d" % c, align_bytes=64)
-            nc.vector.tensor_copy(
-                out=plane[:].rearrange("p (a s m) -> p s a m", a=PASSES, s=PACK),
-                in_=plane_raw[:].rearrange("p (a c m s) -> p c s a m", a=PASSES, c=CHUNKS, s=PACK)[:, c],
-            )
-            return plane
+        w_scales = {}
 
-        def permute_words(c):
-            codes = keep.tile([P, PASSES * WIDE], U32, name="w_codes%d" % c, align_bytes=64)
+        def permute_scales(c, a0, a1):
+            plane = keep.tile([P, (a1 - a0) * WIDE], U8, name="w_scales%d_%d" % (c, a0), align_bytes=64)
             nc.vector.tensor_copy(
-                out=codes[:].bitcast(I32).rearrange("p (a s g i) -> p g a s i", a=PASSES, s=PACK, i=4),
-                in_=w_raw[:, :, c * WIDE : (c + 1) * WIDE].rearrange("p a (g i s) -> p g a s i", s=PACK, i=4),
+                out=plane[:].rearrange("p (a s m) -> p s a m", a=a1 - a0, s=PACK),
+                in_=plane_raw[:].rearrange("p (a c m s) -> p c s a m", a=PASSES, c=CHUNKS, s=PACK)[:, c, :, a0:a1, :],
             )
-            return codes
+            for a in range(a0, a1):
+                w_scales[c, a] = plane[:, (a - a0) * WIDE : (a - a0 + 1) * WIDE]
+
+        w_codes = {}
+
+        def permute_words(c, a, copy, word):
+            codes = keep.tile([P, WIDE], U32, name="w_codes%d_%d" % (c, a), align_bytes=64)
+            copy(
+                out=codes[:].bitcast(word).rearrange("p (s g i) -> p g s i", s=PACK, i=4),
+                in_=w_raw[a][:, c * WIDE : (c + 1) * WIDE].bitcast(word).rearrange("p (g i s) -> p g s i", s=PACK, i=4),
+            )
+            w_codes[c, a] = codes
 
         def load_res(c):
             res_sb = keep.tile([P, TILES, T], F32, name="res%d" % c, align_bytes=256)
@@ -139,24 +143,25 @@ def tile_mix_lrbwd_res_kernel(tc, dy, w8_words, w8_scales, bu, ad, res, out_0, o
             return res_sb
 
         bu_raw = load_passes("bu_raw", bu)
-        w_raw = load_w()
+        ad_raw = load_rows("ad_raw", ad)
+        w_raw = [load_w(0)]
+        load_scales(nc.sync)
 
         dy_q = []
         for a in range(PASSES):
             dy_q.append(quantize("dy%d" % a, interleave(dy_raw[a], SCALAR_COLS_DY), E5M2))
         acc = {}
 
-        def base(c, i):
-            acc[c, i] = bank(TILES * ((c + 1) % 2) + i)
-            for a in range(PASSES):
-                w0 = a * WIDE + i * P
-                mx_pass(acc[c, i], w_codes[c][:, w0 : w0 + P], w_scales[c][:, w0 : w0 + P], dy_q[a], a == 0, False)
+        def base(c, i, a):
+            cols = slice(i * P, (i + 1) * P)
+            mx_pass(acc[c, i], w_codes[c, a][:, cols], w_scales[c, a][:, cols], dy_q[a], False, a == PASSES - 1)
 
         def group_ad(c, scalar_cols):
             return interleave_permuted(ad_raw[:, :, c * WIDE : (c + 1) * WIDE], scalar_cols)
 
         def adapter(c, i):
-            mx_pass(acc[c, i], ad_q[c][i][0], ad_q[c][i][1], h_q, False, True)
+            acc[c, i] = bank(TILES * ((c + 1) % 2) + i)
+            mx_pass(acc[c, i], ad_q[c][i][0], ad_q[c][i][1], h_q, True, False)
 
         def add_res(c, i):
             nc.vector.tensor_tensor(out=sums[c][:, i, :], in0=acc[c, i][:], in1=sums[c][:, i, :], op=mybir.AluOpType.add)
@@ -181,46 +186,48 @@ def tile_mix_lrbwd_res_kernel(tc, dy, w8_words, w8_scales, bu, ad, res, out_0, o
                 nc.scalar.copy(out=h_sb[:, s, :], in_=h_acc[s][:])
             else:
                 nc.vector.tensor_copy(out=h_sb[:, s, :], in_=h_acc[s][:])
-        nc.sync.dma_start(out=out_1.rearrange("(p j) t -> p j t", j=PACK), in_=h_sb[:], max_dma_last_dim=4096)
-        load_scales(nc.scalar)
-        ad_raw = load_rows("ad_raw", ad)
-        sums = [load_res(c) for c in range(CHUNKS)]
-        h_grouped = interleave(h_sb[:], SCALAR_COLS_HALF)
-        w_codes = [permute_words(0)]
-        h_q = quantize("h", h_grouped, E5M2)
-        w_codes.append(permute_words(1))
-        w_scales = [permute_scales(0), permute_scales(1)]
-        w_codes.append(permute_words(last))
-        w_scales.append(permute_scales(last))
+        h_rows = out_1.rearrange("(p j) t -> p j t", j=PACK)
+        nc.sync.dma_start(out=h_rows[:, : PACK // 2, :], in_=h_sb[:, : PACK // 2, :])
+        h_q = quantize("h", interleave(h_sb[:], SCALAR_COLS), E5M2)
 
+        ad_q = [quantize_in_halves("ad0", ad_raw[:, :, :WIDE])]
+        w_raw.extend([load_w(a) for a in range(1, PASSES)])
+        sums = [load_res(c) for c in range(CHUNKS)]
+        nc.sync.dma_start(out=h_rows[:, PACK // 2 :, :], in_=h_sb[:, PACK // 2 :, :])
+        permute_words(0, 0, nc.vector.tensor_copy, I32)
+        grouped = [group_ad(1, SCALAR_COLS_AD), group_ad(last, WIDE)]
+        ad_q.append(stationary_tiles(quantize("ad1", grouped[0], E4M3)))
         for c in range(last):
             for i in range(TILES):
-                base(c, i)
-        ad_q = [quantize_in_halves("ad0", ad_raw[:, :, :WIDE])]
-        grouped = [group_ad(1, SCALAR_COLS_AD), group_ad(last, WIDE)]
+                adapter(c, i)
+        permute_scales(0, 0, 1)
+        permute_scales(0, 1, PASSES)
+        permute_words(0, 1, nc.vector.tensor_copy, I32)
+        permute_scales(1, 0, PASSES)
+        permute_words(0, PASSES - 1, nc.vector.tensor_copy, I32)
+        for c in range(1, CHUNKS):
+            for a in range(PASSES):
+                permute_words(c, a, nc.scalar.copy, U32)
+        permute_scales(last, 0, PASSES)
+        ad_q.append(stationary_tiles(quantize("ad2", grouped[1], E4M3)))
+        for a in range(PASSES):
+            for i in range(TILES):
+                base(0, i, a)
         for i in range(TILES):
-            adapter(0, i)
-        for i in range(TILES - 1):
+            for a in range(PASSES):
+                base(1, i, a)
+        for i in range(TILES):
             add_res(0, i)
-        for i in range(TILES // 2):
-            base(last, i)
-        ad_q.append(stationary_tiles(quantize("ad1", grouped[0], E4M3)))
-        for i in range(TILES):
-            adapter(1, i)
-        add_res(0, TILES - 1)
-        for i in range(TILES // 2, TILES):
-            base(last, i)
         store(0, 0, TILES)
-        for i in range(TILES - 1):
-            add_res(1, i)
-        half = WIDE * PACK // 2
-        ad_q.append(stationary_tiles(quantize("ad2_0", grouped[1][:, :half], E4M3)))
-        add_res(1, TILES - 1)
-        store(1, 0, TILES)
-        ad_q[last].extend(stationary_tiles(quantize("ad2_1", grouped[1][:, half:], E4M3)))
         for i in range(TILES):
             adapter(last, i)
-        for i0 in range(0, TILES, 2):
-            add_res(last, i0)
-            add_res(last, i0 + 1)
-            store(last, i0, i0 + 2)
+            for a in range(PASSES):
+                base(last, i, a)
+        for i in range(TILES):
+            add_res(1, i)
+        store(1, 0, TILES)
+        for i in range(TILES - 1):
+            add_res(last, i)
+        store(last, 0, TILES - 1)
+        add_res(last, TILES - 1)
+        store(last, TILES - 1, TILES)

@@ -17,13 +17,15 @@ P = 128
 PACK = 4
 K_PASS = P * PACK
 PASSES = N // K_PASS
-WIDE = 512
+ROWS = 3
+WIDE = ROWS * P
 CHUNKS = K // WIDE
-TILES = WIDE // P
-SCALAR_COLS = 192
-SCALAR_COLS_HALF = 256
-SCALAR_COLS_DY = 320
-SCALAR_COLS_AD = 384
+BANKS = 8
+LINE = 4
+SCALAR_DY = 320
+SCALAR_H = 192
+SCALAR_BU = 48
+SCALAR_AD = (44, 64, P, P)
 
 
 def tile_mix_lrbwd_res_kernel(tc, dy, w8_words, w8_scales, bu, ad, res, out_0, out_1):
@@ -35,10 +37,34 @@ def tile_mix_lrbwd_res_kernel(tc, dy, w8_words, w8_scales, bu, ad, res, out_0, o
         psum = ctx.enter_context(tc.psum_pool(name="psum", bufs=1))
         ctx.enter_context(tc.manual_schedule())
 
-        def load_rows(name, rows):
-            raw = keep.tile([P, PACK, rows.shape[1]], F32, name=name, align_bytes=256)
-            nc.sync.dma_start(out=raw[:], in_=rows.rearrange("(p j) w -> p j w", j=PACK))
+        def load_rows(name, rows, per_partition):
+            raw = keep.tile([P, per_partition, rows.shape[1]], F32, name=name, align_bytes=256)
+            nc.sync.dma_start(out=raw[:], in_=rows.rearrange("(p j) w -> p j w", j=per_partition))
             return raw
+
+        def load_passes(name, rows):
+            return [load_rows("%s%d" % (name, a), rows[a * K_PASS : (a + 1) * K_PASS, :], PACK)[:] for a in range(PASSES)]
+
+        def load_words(a):
+            words = keep.tile([P, K], I32, name="w_raw%d" % a, align_bytes=256)
+            nc.sync.dma_start(out=words[:], in_=w8_words[a].rearrange("p n i -> p (n i)").bitcast(I32))
+            return words
+
+        def share(dst, src, cut):
+            nc.scalar.copy(out=dst[:, :cut], in_=src[:, :cut])
+            if cut < dst.shape[1]:
+                nc.vector.tensor_copy(out=dst[:, cut:], in_=src[:, cut:])
+
+        def interleave(raw, scalar_cols):
+            grouped = stage.tile([P, T * PACK], BF16, name="grouped", align_bytes=64)
+            dst = grouped[:].rearrange("p (c i j) -> p c j i", i=LINE, j=PACK)
+            share(dst, raw.rearrange("p j (c i) -> p c j i", i=LINE), scalar_cols // LINE)
+            return grouped[:]
+
+        def interleave_permuted(grouped, raw, tiles, scalar_m):
+            dst = grouped.rearrange("p (s m j) -> p m j s", s=tiles, j=PACK)
+            share(dst, raw.rearrange("p j (m s) -> p m j s", s=tiles), scalar_m)
+            return grouped
 
         def quantize(name, grouped, fmt):
             codes = keep.tile([P, grouped.shape[1] // PACK], U32, name=name + "_codes", align_bytes=64)
@@ -46,188 +72,151 @@ def tile_mix_lrbwd_res_kernel(tc, dy, w8_words, w8_scales, bu, ad, res, out_0, o
             nc.vector.quantize_mx(out=codes[:].bitcast(fmt), scales=scales[:], in_=grouped)
             return codes, scales
 
-        def interleave(raw, scalar_cols):
-            grouped = stage.tile([P, WIDE * PACK], BF16, name="grouped", align_bytes=64)
-            dst = grouped[:].rearrange("p (c i j) -> p c j i", i=4, j=PACK)
-            src = raw.rearrange("p j (c i) -> p c j i", i=4)
-            cut = scalar_cols // 4
-            nc.scalar.copy(out=dst[:, :cut], in_=src[:, :cut])
-            nc.vector.tensor_copy(out=dst[:, cut:], in_=src[:, cut:])
-            return grouped[:]
-
-        def interleave_permuted(raw, scalar_cols):
-            grouped = stage.tile([P, WIDE * PACK], BF16, name="grouped", align_bytes=64)
-            dst = grouped[:].rearrange("p (s m j) -> p m j s", s=PACK, j=PACK)
-            src = raw.rearrange("p j (m s) -> p m j s", s=PACK)
-            cut = scalar_cols // 4
-            nc.scalar.copy(out=dst[:, :cut], in_=src[:, :cut])
-            if scalar_cols < WIDE:
-                nc.vector.tensor_copy(out=dst[:, cut:], in_=src[:, cut:])
-            return grouped[:]
-
-        def stationary_tiles(quantized):
-            codes, scales = quantized
+        def stationary_tiles(codes, scales):
             return [(codes[:, m0 : m0 + P], scales[:, m0 : m0 + P]) for m0 in range(0, codes.shape[1], P)]
 
-        def quantize_in_halves(name, raw):
-            src = raw.rearrange("p j (m u s) -> p u m j s", u=2, s=2)
-            halves = []
-            for u, copy in enumerate((nc.vector.tensor_copy, nc.scalar.copy)):
-                half = keep.tile([P, WIDE * PACK // 2], BF16, name="%s_half%d" % (name, u), align_bytes=64)
-                copy(out=half[:].rearrange("p (s m j) -> p m j s", s=2, j=PACK), in_=src[:, u])
-                halves.append(half[:])
-            tiles = []
-            for u, half in enumerate(halves):
-                tiles.extend(stationary_tiles(quantize("%s_%d" % (name, u), half, E4M3)))
-            return tiles
-
-        def mx_pass(acc, codes, scales, rhs, start, stop):
+        def mx_pass(acc, stationary, moving, start, stop):
             nc.tensor.matmul_mx(
                 out=acc[:],
-                lhsT=codes.bitcast(E4M3),
-                lhsT_scale=scales,
-                rhs=rhs[0][:].bitcast(E5M2),
-                rhs_scale=rhs[1][:],
+                lhsT=stationary[0].bitcast(E4M3),
+                lhsT_scale=stationary[1],
+                rhs=moving[0][:].bitcast(E5M2),
+                rhs_scale=moving[1][:],
                 start=start,
                 stop=stop,
             )
 
         def bank(b):
-            acc = psum.tile([P, WIDE], F32, name="bank%d" % b)
+            acc = psum.tile([P, T], F32, name="bank%d" % b)
             return acc
 
         plane_raw = keep.tile([P, PASSES * K], U8, name="plane_raw", align_bytes=256)
         nc.vector.memset(plane_raw[:].bitcast(I32), 0)
-
-        def load_passes(name, rows):
-            return [load_rows("%s%d" % (name, a), rows[a * K_PASS : (a + 1) * K_PASS, :])[:] for a in range(PASSES)]
-
-        def load_scales(queue):
-            for r in range(4):
-                queue.dma_start(
-                    out=plane_raw[r:P:32, :].bitcast(I32).rearrange("q (a n) -> q a n", a=PASSES),
-                    in_=w8_scales[:, r:16:4, :].bitcast(I32).rearrange("a q n -> q a n"),
-                )
-
         dy_raw = load_passes("dy_raw", dy)
-
-        def load_w(a):
-            words = keep.tile([P, K], I32, name="w_raw%d" % a, align_bytes=256)
-            nc.sync.dma_start(out=words[:], in_=w8_words[a].rearrange("p n i -> p (n i)").bitcast(I32))
-            return words
-
-        w_scales = {}
-
-        def permute_scales(c, a0, a1):
-            plane = keep.tile([P, (a1 - a0) * WIDE], U8, name="w_scales%d_%d" % (c, a0), align_bytes=64)
-            nc.vector.tensor_copy(
-                out=plane[:].rearrange("p (a s m) -> p s a m", a=a1 - a0, s=PACK),
-                in_=plane_raw[:].rearrange("p (a c m s) -> p c s a m", a=PASSES, c=CHUNKS, s=PACK)[:, c, :, a0:a1, :],
+        bu_raw = load_passes("bu_raw", bu)
+        ad_raw = load_rows("ad_raw", ad, PACK)
+        w_raw = [load_words(0)]
+        for r in range(4):
+            nc.sync.dma_start(
+                out=plane_raw[r:P:32, :].bitcast(I32).rearrange("q (a n) -> q a n", a=PASSES),
+                in_=w8_scales[:, r:16:4, :].bitcast(I32).rearrange("a q n -> q a n"),
             )
-            for a in range(a0, a1):
-                w_scales[c, a] = plane[:, (a - a0) * WIDE : (a - a0 + 1) * WIDE]
 
-        w_codes = {}
+        dy_q = [quantize("dy%d" % a, interleave(dy_raw[a], SCALAR_DY), E5M2) for a in range(PASSES)]
+        h_acc = [bank(s) for s in range(PACK)]
+        for a in range(PASSES):
+            if a < PASSES - 1:
+                grouped = stage.tile([P, R * PACK], BF16, name="grouped", align_bytes=64)
+                bu_q = stationary_tiles(*quantize("bu%d" % a, interleave_permuted(grouped[:], bu_raw[a], PACK, SCALAR_BU), E4M3))
+            else:
+                src = bu_raw[a].rearrange("p j (m u s) -> p u m j s", u=2, s=2)
+                halves = []
+                for u, copy in enumerate((nc.vector.tensor_copy, nc.scalar.copy)):
+                    half = keep.tile([P, R * PACK // 2], BF16, name="bu_half%d" % u, align_bytes=64)
+                    copy(out=half[:].rearrange("p (s m j) -> p m j s", s=2, j=PACK), in_=src[:, u])
+                    halves.append(half[:])
+                bu_q = []
+                for u, half in enumerate(halves):
+                    bu_q.extend(stationary_tiles(*quantize("bu%d_%d" % (a, u), half, E4M3)))
+            for s in range(PACK):
+                mx_pass(h_acc[s], bu_q[s], dy_q[a], a == 0, a == PASSES - 1)
+        h_sb = keep.tile([P, PACK, T], F32, name="h_sb", align_bytes=256)
+        for s in range(PACK):
+            copy = nc.scalar.copy if s % 2 == 1 else nc.vector.tensor_copy
+            copy(out=h_sb[:, s, :], in_=h_acc[s][:])
+        nc.sync.dma_start(out=out_1.rearrange("(p j) t -> p j t", j=PACK), in_=h_sb[:])
+        h_q = quantize("h", interleave(h_sb[:], SCALAR_H), E5M2)
+
+        w_raw.extend([load_words(a) for a in range(1, PASSES)])
+        sums = [load_rows("res%d" % c, res[c * WIDE : (c + 1) * WIDE, :], ROWS) for c in range(CHUNKS)]
+
+        ad_grouped, ad_q, w_codes, w_planes, acc = {}, {}, {}, {}, {}
+
+        def group_ad(c):
+            grouped = keep.tile([P, WIDE * PACK], BF16, name="ad_grouped%d" % c, align_bytes=64)
+            ad_grouped[c] = interleave_permuted(grouped[:], ad_raw[:, :, c * WIDE : (c + 1) * WIDE], ROWS, SCALAR_AD[c])
+
+        def quantize_ad(c):
+            ad_q[c] = stationary_tiles(*quantize("ad%d" % c, ad_grouped[c], E4M3))
 
         def permute_words(c, a, copy, word):
             codes = keep.tile([P, WIDE], U32, name="w_codes%d_%d" % (c, a), align_bytes=64)
             copy(
-                out=codes[:].bitcast(word).rearrange("p (s g i) -> p g s i", s=PACK, i=4),
-                in_=w_raw[a][:, c * WIDE : (c + 1) * WIDE].bitcast(word).rearrange("p (g i s) -> p g s i", s=PACK, i=4),
+                out=codes[:].bitcast(word).rearrange("p (s g i) -> p g s i", s=ROWS, i=LINE),
+                in_=w_raw[a][:, c * WIDE : (c + 1) * WIDE].bitcast(word).rearrange("p (g i s) -> p g s i", s=ROWS, i=LINE),
             )
             w_codes[c, a] = codes
 
-        def load_res(c):
-            res_sb = keep.tile([P, TILES, T], F32, name="res%d" % c, align_bytes=256)
-            nc.sync.dma_start(out=res_sb[:], in_=res[c * WIDE : (c + 1) * WIDE, :].rearrange("(p s) t -> p s t", s=PACK))
-            return res_sb
+        def words_by_vector(c, a):
+            permute_words(c, a, nc.vector.tensor_copy, I32)
 
-        bu_raw = load_passes("bu_raw", bu)
-        ad_raw = load_rows("ad_raw", ad)
-        w_raw = [load_w(0)]
-        load_scales(nc.sync)
+        def words_by_scalar(c, a):
+            permute_words(c, a, nc.scalar.copy, U32)
 
-        dy_q = []
-        for a in range(PASSES):
-            dy_q.append(quantize("dy%d" % a, interleave(dy_raw[a], SCALAR_COLS_DY), E5M2))
-        acc = {}
+        def permute_plane(c, a0, a1):
+            plane = keep.tile([P, (a1 - a0) * WIDE], U8, name="w_plane%d_%d" % (c, a0), align_bytes=64)
+            src = plane_raw[:].rearrange("p (a c u m s) -> p c u a s m", a=PASSES, c=CHUNKS, u=2, s=ROWS)
+            nc.vector.tensor_copy(
+                out=plane[:].rearrange("p (a s u m) -> p u a s m", a=a1 - a0, s=ROWS, u=2), in_=src[:, c, :, a0:a1]
+            )
+            for a in range(a0, a1):
+                w_planes[c, a] = plane[:, (a - a0) * WIDE : (a - a0 + 1) * WIDE]
 
-        def base(c, i, a):
-            cols = slice(i * P, (i + 1) * P)
-            mx_pass(acc[c, i], w_codes[c, a][:, cols], w_scales[c, a][:, cols], dy_q[a], False, a == PASSES - 1)
+        def adapter(i):
+            c, s = divmod(i, ROWS)
+            acc[i] = bank((i + PACK) % BANKS)
+            mx_pass(acc[i], ad_q[c][s], h_q, True, False)
 
-        def group_ad(c, scalar_cols):
-            return interleave_permuted(ad_raw[:, :, c * WIDE : (c + 1) * WIDE], scalar_cols)
+        def base(i, a):
+            c, s = divmod(i, ROWS)
+            cols = slice(s * P, (s + 1) * P)
+            mx_pass(acc[i], (w_codes[c, a][:, cols], w_planes[c, a][:, cols]), dy_q[a], False, a == PASSES - 1)
 
-        def adapter(c, i):
-            acc[c, i] = bank(TILES * ((c + 1) % 2) + i)
-            mx_pass(acc[c, i], ad_q[c][i][0], ad_q[c][i][1], h_q, True, False)
+        def add_res(i):
+            c, s = divmod(i, ROWS)
+            nc.vector.tensor_tensor(out=sums[c][:, s, :], in0=acc[i][:], in1=sums[c][:, s, :], op=mybir.AluOpType.add)
+            if s == ROWS - 1:
+                rows = out_0[c * WIDE : (c + 1) * WIDE, :].rearrange("(p s) t -> p s t", s=ROWS)
+                nc.sync.dma_start(out=rows, in_=sums[c][:])
 
-        def add_res(c, i):
-            nc.vector.tensor_tensor(out=sums[c][:, i, :], in0=acc[c, i][:], in1=sums[c][:, i, :], op=mybir.AluOpType.add)
+        for c in range(CHUNKS):
+            group_ad(c)
+        quantize_ad(0)
+        quantize_ad(1)
+        words_by_vector(0, 0)
+        words_by_vector(1, 0)
+        permute_plane(0, 0, 1)
+        permute_plane(1, 0, 1)
+        words_by_vector(2, 0)
+        quantize_ad(2)
+        permute_plane(2, 0, 1)
+        for c in range(CHUNKS - 1):
+            permute_plane(c, 1, PASSES)
+        words_by_scalar(3, 0)
+        for a in range(1, PASSES):
+            words_by_vector(0, a)
+            words_by_vector(1, a)
+            words_by_scalar(2, a)
+            words_by_scalar(3, a)
+            if a == 1:
+                quantize_ad(3)
+                permute_plane(3, 0, PASSES)
 
-        def store(c, i0, i1):
-            rows = out_0[c * WIDE : (c + 1) * WIDE, :].rearrange("(p s) t -> p s t", s=PACK)
-            nc.sync.dma_start(out=rows[:, i0:i1, :], in_=sums[c][:, i0:i1, :])
-
-        last = CHUNKS - 1
-
-        h_acc = [bank(s) for s in range(PACK)]
-        for a in range(PASSES):
-            if a == PASSES - 1:
-                bu_q = quantize_in_halves("bu%d" % a, bu_raw[a])
-            else:
-                bu_q = stationary_tiles(quantize("bu%d" % a, interleave_permuted(bu_raw[a], SCALAR_COLS), E4M3))
-            for s in range(PACK):
-                mx_pass(h_acc[s], bu_q[s][0], bu_q[s][1], dy_q[a], a == 0, a == PASSES - 1)
-        h_sb = keep.tile([P, PACK, T], F32, name="h_sb", align_bytes=256)
-        for s in range(PACK):
-            if s % 2 == 1:
-                nc.scalar.copy(out=h_sb[:, s, :], in_=h_acc[s][:])
-            else:
-                nc.vector.tensor_copy(out=h_sb[:, s, :], in_=h_acc[s][:])
-        h_rows = out_1.rearrange("(p j) t -> p j t", j=PACK)
-        nc.sync.dma_start(out=h_rows[:, : PACK // 2, :], in_=h_sb[:, : PACK // 2, :])
-        h_q = quantize("h", interleave(h_sb[:], SCALAR_COLS), E5M2)
-
-        ad_q = [quantize_in_halves("ad0", ad_raw[:, :, :WIDE])]
-        w_raw.extend([load_w(a) for a in range(1, PASSES)])
-        sums = [load_res(c) for c in range(CHUNKS)]
-        nc.sync.dma_start(out=h_rows[:, PACK // 2 :, :], in_=h_sb[:, PACK // 2 :, :])
-        permute_words(0, 0, nc.vector.tensor_copy, I32)
-        grouped = [group_ad(1, SCALAR_COLS_AD), group_ad(last, WIDE)]
-        ad_q.append(stationary_tiles(quantize("ad1", grouped[0], E4M3)))
-        for c in range(last):
-            for i in range(TILES):
-                adapter(c, i)
-        permute_scales(0, 0, 1)
-        permute_scales(0, 1, PASSES)
-        permute_words(0, 1, nc.vector.tensor_copy, I32)
-        permute_scales(1, 0, PASSES)
-        permute_words(0, PASSES - 1, nc.vector.tensor_copy, I32)
-        for c in range(1, CHUNKS):
-            for a in range(PASSES):
-                permute_words(c, a, nc.scalar.copy, U32)
-        permute_scales(last, 0, PASSES)
-        ad_q.append(stationary_tiles(quantize("ad2", grouped[1], E4M3)))
-        for a in range(PASSES):
-            for i in range(TILES):
-                base(0, i, a)
-        for i in range(TILES):
-            for a in range(PASSES):
-                base(1, i, a)
-        for i in range(TILES):
-            add_res(0, i)
-        store(0, 0, TILES)
-        for i in range(TILES):
-            adapter(last, i)
-            for a in range(PASSES):
-                base(last, i, a)
-        for i in range(TILES):
-            add_res(1, i)
-        store(1, 0, TILES)
-        for i in range(TILES - 1):
-            add_res(last, i)
-        store(last, 0, TILES - 1)
-        add_res(last, TILES - 1)
-        store(last, TILES - 1, TILES)
+        two = 2 * ROWS
+        for i in range(two):
+            adapter(i)
+        for i in range(two):
+            base(i, 0)
+        for i in range(two, BANKS):
+            adapter(i)
+        for i in range(two, BANKS):
+            base(i, 0)
+        for a in range(1, PASSES):
+            for i in range(BANKS):
+                base(i, a)
+        for i in range(CHUNKS * ROWS):
+            add_res(i)
+            if i + BANKS < CHUNKS * ROWS:
+                adapter(i + BANKS)
+                for a in range(PASSES):
+                    base(i + BANKS, a)

@@ -25,7 +25,7 @@ LINE = 4
 SCALAR_DY = 320
 SCALAR_H = 192
 SCALAR_BU = 48
-SCALAR_AD = (44, 64, P, P)
+SCALAR_AD = (None, 64, P, P)
 
 
 def tile_mix_lrbwd_res_kernel(tc, dy, w8_words, w8_scales, bu, ad, res, out_0, out_1):
@@ -179,16 +179,30 @@ def tile_mix_lrbwd_res_kernel(tc, dy, w8_words, w8_scales, bu, ad, res, out_0, o
                 rows = out_0[c * WIDE : (c + 1) * WIDE, :].rearrange("(p s) t -> p s t", s=ROWS)
                 nc.sync.dma_start(out=rows, in_=sums[c][:])
 
-        for c in range(CHUNKS):
+        def group_ad_tile(s, copy):
+            grouped = keep.tile([P, P * PACK], BF16, name="ad_tile%d" % s, align_bytes=64)
+            copy(
+                out=grouped[:].rearrange("p (m j) -> p m j", j=PACK),
+                in_=ad_raw[:, :, :WIDE].rearrange("p j (m s) -> p s m j", s=ROWS)[:, s],
+            )
+            return grouped[:]
+
+        def quantize_ad_tile(s, grouped):
+            return stationary_tiles(*quantize("ad0_%d" % s, grouped, E4M3))
+
+        second = group_ad_tile(1, nc.scalar.copy)
+        ad_q[0] = quantize_ad_tile(0, group_ad_tile(0, nc.vector.tensor_copy))
+        third = group_ad_tile(2, nc.vector.tensor_copy)
+        ad_q[0] = ad_q[0] + quantize_ad_tile(1, second) + quantize_ad_tile(2, third)
+        for c in range(1, CHUNKS):
             group_ad(c)
-        quantize_ad(0)
         quantize_ad(1)
         words_by_vector(0, 0)
-        words_by_vector(1, 0)
         permute_plane(0, 0, 1)
+        words_by_vector(1, 0)
         permute_plane(1, 0, 1)
-        words_by_vector(2, 0)
         quantize_ad(2)
+        words_by_vector(2, 0)
         permute_plane(2, 0, 1)
         for c in range(CHUNKS - 1):
             permute_plane(c, 1, PASSES)

@@ -17,10 +17,12 @@ P = 128
 PACK = 4
 K_PASS = P * PACK
 PASSES = N // K_PASS
-ROWS = 3
-WIDE = ROWS * P
-CHUNKS = K // WIDE
+ROWS = (3, 3, 4, 2)
+CHUNKS = len(ROWS)
+FIRST = tuple(sum(ROWS[:c]) for c in range(CHUNKS))
+TILES = tuple((c, s) for c in range(CHUNKS) for s in range(ROWS[c]))
 BANKS = 8
+WARM_UP = 6
 LINE = 4
 SCALAR_DY = 320
 SCALAR_H = 192
@@ -36,6 +38,9 @@ def tile_mix_lrbwd_res_kernel(tc, dy, w8_words, w8_scales, bu, ad, res, out_0, o
         stage = ctx.enter_context(tc.tile_pool(name="stage", bufs=3))
         psum = ctx.enter_context(tc.psum_pool(name="psum", bufs=1))
         ctx.enter_context(tc.manual_schedule())
+
+        def chunk_cols(c):
+            return slice(FIRST[c] * P, (FIRST[c] + ROWS[c]) * P)
 
         def load_rows(name, rows, per_partition):
             raw = keep.tile([P, per_partition, rows.shape[1]], F32, name=name, align_bytes=256)
@@ -122,28 +127,30 @@ def tile_mix_lrbwd_res_kernel(tc, dy, w8_words, w8_scales, bu, ad, res, out_0, o
                 mx_pass(h_acc[s], bu_q[s], dy_q[a], a == 0, a == PASSES - 1)
         h_sb = keep.tile([P, PACK, T], F32, name="h_sb", align_bytes=256)
         for s in range(PACK):
-            copy = nc.scalar.copy if s % 2 == 1 else nc.vector.tensor_copy
-            copy(out=h_sb[:, s, :], in_=h_acc[s][:])
+            nc.scalar.copy(out=h_sb[:, s, :], in_=h_acc[s][:])
+        idle = bank(PACK - 1)
+        for i in range(WARM_UP):
+            mx_pass(idle, bu_q[0], dy_q[PASSES - 1], True, True)
         nc.sync.dma_start(out=out_1.rearrange("(p j) t -> p j t", j=PACK), in_=h_sb[:])
         h_q = quantize("h", interleave(h_sb[:], SCALAR_H), E5M2)
 
         w_raw.extend([load_words(a) for a in range(1, PASSES)])
-        sums = [load_rows("res%d" % c, res[c * WIDE : (c + 1) * WIDE, :], ROWS) for c in range(CHUNKS)]
+        sums = [load_rows("res%d" % c, res[chunk_cols(c), :], ROWS[c]) for c in range(CHUNKS)]
 
         ad_grouped, ad_q, w_codes, w_planes, acc = {}, {}, {}, {}, {}
 
         def group_ad(c):
-            grouped = keep.tile([P, WIDE * PACK], BF16, name="ad_grouped%d" % c, align_bytes=64)
-            ad_grouped[c] = interleave_permuted(grouped[:], ad_raw[:, :, c * WIDE : (c + 1) * WIDE], ROWS, SCALAR_AD[c])
+            grouped = keep.tile([P, ROWS[c] * P * PACK], BF16, name="ad_grouped%d" % c, align_bytes=64)
+            ad_grouped[c] = interleave_permuted(grouped[:], ad_raw[:, :, chunk_cols(c)], ROWS[c], SCALAR_AD[c])
 
         def quantize_ad(c):
             ad_q[c] = stationary_tiles(*quantize("ad%d" % c, ad_grouped[c], E4M3))
 
         def permute_words(c, a, copy, word):
-            codes = keep.tile([P, WIDE], U32, name="w_codes%d_%d" % (c, a), align_bytes=64)
+            codes = keep.tile([P, ROWS[c] * P], U32, name="w_codes%d_%d" % (c, a), align_bytes=64)
             copy(
-                out=codes[:].bitcast(word).rearrange("p (s g i) -> p g s i", s=ROWS, i=LINE),
-                in_=w_raw[a][:, c * WIDE : (c + 1) * WIDE].bitcast(word).rearrange("p (g i s) -> p g s i", s=ROWS, i=LINE),
+                out=codes[:].bitcast(word).rearrange("p (s g i) -> p g s i", s=ROWS[c], i=LINE),
+                in_=w_raw[a][:, chunk_cols(c)].bitcast(word).rearrange("p (g i s) -> p g s i", s=ROWS[c], i=LINE),
             )
             w_codes[c, a] = codes
 
@@ -153,37 +160,45 @@ def tile_mix_lrbwd_res_kernel(tc, dy, w8_words, w8_scales, bu, ad, res, out_0, o
         def words_by_scalar(c, a):
             permute_words(c, a, nc.scalar.copy, U32)
 
-        def permute_plane(c, a0, a1):
-            plane = keep.tile([P, (a1 - a0) * WIDE], U8, name="w_plane%d_%d" % (c, a0), align_bytes=64)
-            src = plane_raw[:].rearrange("p (a c u m s) -> p c u a s m", a=PASSES, c=CHUNKS, u=2, s=ROWS)
+        def permute_planes(c, a0, a1):
+            wide = ROWS[c] * P
+            plane = keep.tile([P, (a1 - a0) * wide], U8, name="w_plane%d_%d" % (c, a0), align_bytes=64)
+            src = plane_raw[:].rearrange("p (a k) -> p a k", a=PASSES)[:, a0:a1, chunk_cols(c)]
             nc.vector.tensor_copy(
-                out=plane[:].rearrange("p (a s u m) -> p u a s m", a=a1 - a0, s=ROWS, u=2), in_=src[:, c, :, a0:a1]
+                out=plane[:].rearrange("p (a s u m) -> p u a s m", a=a1 - a0, s=ROWS[c], u=2),
+                in_=src.rearrange("p a (u m s) -> p u a s m", u=2, s=ROWS[c]),
             )
             for a in range(a0, a1):
-                w_planes[c, a] = plane[:, (a - a0) * WIDE : (a - a0 + 1) * WIDE]
+                w_planes[c, a] = plane[:, (a - a0) * wide : (a - a0 + 1) * wide]
 
         def adapter(i):
-            c, s = divmod(i, ROWS)
+            c, s = TILES[i]
             acc[i] = bank((i + PACK) % BANKS)
             mx_pass(acc[i], ad_q[c][s], h_q, True, False)
 
         def base(i, a):
-            c, s = divmod(i, ROWS)
+            c, s = TILES[i]
             cols = slice(s * P, (s + 1) * P)
             mx_pass(acc[i], (w_codes[c, a][:, cols], w_planes[c, a][:, cols]), dy_q[a], False, a == PASSES - 1)
 
         def add_res(i):
-            c, s = divmod(i, ROWS)
+            c, s = TILES[i]
             nc.vector.tensor_tensor(out=sums[c][:, s, :], in0=acc[i][:], in1=sums[c][:, s, :], op=mybir.AluOpType.add)
-            if s == ROWS - 1:
-                rows = out_0[c * WIDE : (c + 1) * WIDE, :].rearrange("(p s) t -> p s t", s=ROWS)
-                nc.sync.dma_start(out=rows, in_=sums[c][:])
+
+        def add_res_beside(i):
+            c, s = TILES[i]
+            dx = keep.tile([P, T], F32, name="dx", align_bytes=64)
+            nc.scalar.copy(out=dx[:], in_=acc[i][:])
+            nc.gpsimd.tensor_tensor(out=sums[c][:, s, :], in0=dx[:], in1=sums[c][:, s, :], op=mybir.AluOpType.add)
+
+        def store(c):
+            nc.sync.dma_start(out=out_0[chunk_cols(c), :].rearrange("(p s) t -> p s t", s=ROWS[c]), in_=sums[c][:])
 
         def group_ad_tile(s, copy):
             grouped = keep.tile([P, P * PACK], BF16, name="ad_tile%d" % s, align_bytes=64)
             copy(
                 out=grouped[:].rearrange("p (m j) -> p m j", j=PACK),
-                in_=ad_raw[:, :, :WIDE].rearrange("p j (m s) -> p s m j", s=ROWS)[:, s],
+                in_=ad_raw[:, :, chunk_cols(0)].rearrange("p j (m s) -> p s m j", s=ROWS[0])[:, s],
             )
             return grouped[:]
 
@@ -194,43 +209,47 @@ def tile_mix_lrbwd_res_kernel(tc, dy, w8_words, w8_scales, bu, ad, res, out_0, o
         ad_q[0] = quantize_ad_tile(0, group_ad_tile(0, nc.vector.tensor_copy))
         third = group_ad_tile(2, nc.vector.tensor_copy)
         ad_q[0] = ad_q[0] + quantize_ad_tile(1, second) + quantize_ad_tile(2, third)
-        for c in range(1, CHUNKS):
-            group_ad(c)
+        last = CHUNKS - 1
+        group_ad(1)
+        group_ad(2)
         quantize_ad(1)
         words_by_vector(0, 0)
-        permute_plane(0, 0, 1)
-        words_by_vector(1, 0)
-        permute_plane(1, 0, 1)
+        for c in range(1, CHUNKS):
+            words_by_scalar(c, 0)
+        group_ad(last)
+        permute_planes(0, 0, 1)
+        permute_planes(1, 0, 1)
+        permute_planes(2, 0, 1)
         quantize_ad(2)
-        words_by_vector(2, 0)
-        permute_plane(2, 0, 1)
-        for c in range(CHUNKS - 1):
-            permute_plane(c, 1, PASSES)
-        words_by_scalar(3, 0)
+        for c in range(last):
+            permute_planes(c, 1, PASSES)
+        permute_planes(last, 0, PASSES)
         for a in range(1, PASSES):
-            words_by_vector(0, a)
-            words_by_vector(1, a)
-            words_by_scalar(2, a)
-            words_by_scalar(3, a)
+            for c in range(CHUNKS):
+                if c < 2:
+                    words_by_vector(c, a)
+                else:
+                    words_by_scalar(c, a)
             if a == 1:
-                quantize_ad(3)
-                permute_plane(3, 0, PASSES)
+                quantize_ad(last)
 
-        two = 2 * ROWS
-        for i in range(two):
-            adapter(i)
-        for i in range(two):
-            base(i, 0)
-        for i in range(two, BANKS):
-            adapter(i)
-        for i in range(two, BANKS):
-            base(i, 0)
-        for a in range(1, PASSES):
-            for i in range(BANKS):
-                base(i, a)
-        for i in range(CHUNKS * ROWS):
-            add_res(i)
-            if i + BANKS < CHUNKS * ROWS:
+        two = FIRST[2]
+        for tiles in (range(two), range(two, BANKS)):
+            for i in tiles:
+                adapter(i)
+            for i in tiles:
+                base(i, 0)
+        for tiles in (range(two), range(two, BANKS)):
+            for a in range(1, PASSES):
+                for i in tiles:
+                    base(i, a)
+        add_res_beside(two)
+        for i, (c, s) in enumerate(TILES):
+            if i != two:
+                add_res(i)
+            if s == ROWS[c] - 1:
+                store(c)
+            if i + BANKS < len(TILES):
                 adapter(i + BANKS)
                 for a in range(PASSES):
                     base(i + BANKS, a)

@@ -22,7 +22,6 @@ CHUNKS = len(ROWS)
 FIRST = tuple(sum(ROWS[:c]) for c in range(CHUNKS))
 TILES = tuple((c, s) for c in range(CHUNKS) for s in range(ROWS[c]))
 BANKS = 8
-WARM_UP = 6
 LINE = 4
 SCALAR_DY = 320
 SCALAR_H = 192
@@ -128,9 +127,6 @@ def tile_mix_lrbwd_res_kernel(tc, dy, w8_words, w8_scales, bu, ad, res, out_0, o
         h_sb = keep.tile([P, PACK, T], F32, name="h_sb", align_bytes=256)
         for s in range(PACK):
             nc.scalar.copy(out=h_sb[:, s, :], in_=h_acc[s][:])
-        idle = bank(PACK - 1)
-        for i in range(WARM_UP):
-            mx_pass(idle, bu_q[0], dy_q[PASSES - 1], True, True)
         nc.sync.dma_start(out=out_1.rearrange("(p j) t -> p j t", j=PACK), in_=h_sb[:])
         h_q = quantize("h", interleave(h_sb[:], SCALAR_H), E5M2)
 

@@ -183,7 +183,7 @@ def tile_mix_lrbwd_res_kernel(tc, dy, w8_words, w8_scales, bu, ad, res, out_0, o
 
         def add_res_beside(i):
             c, s = TILES[i]
-            dx = keep.tile([P, T], F32, name="dx", align_bytes=64)
+            dx = keep.tile([P, T], F32, name="dx%d" % c, align_bytes=64)
             nc.scalar.copy(out=dx[:], in_=acc[i][:])
             nc.gpsimd.tensor_tensor(out=sums[c][:, s, :], in0=dx[:], in1=sums[c][:, s, :], op=mybir.AluOpType.add)
 
@@ -210,24 +210,24 @@ def tile_mix_lrbwd_res_kernel(tc, dy, w8_words, w8_scales, bu, ad, res, out_0, o
         group_ad(2)
         quantize_ad(1)
         words_by_vector(0, 0)
-        for c in range(1, CHUNKS):
-            words_by_scalar(c, 0)
-        group_ad(last)
         permute_planes(0, 0, 1)
+        words_by_vector(1, 0)
         permute_planes(1, 0, 1)
         permute_planes(2, 0, 1)
         quantize_ad(2)
-        for c in range(last):
-            permute_planes(c, 1, PASSES)
-        permute_planes(last, 0, PASSES)
         for a in range(1, PASSES):
-            for c in range(CHUNKS):
-                if c < 2:
-                    words_by_vector(c, a)
-                else:
-                    words_by_scalar(c, a)
-            if a == 1:
-                quantize_ad(last)
+            for c in range(2):
+                permute_planes(c, a, a + 1)
+            for c in range(2):
+                words_by_vector(c, a)
+        permute_planes(2, 1, PASSES)
+        words_by_scalar(2, 0)
+        group_ad(last)
+        quantize_ad(last)
+        words_by_scalar(last, 0)
+        for a in range(1, PASSES):
+            for c in range(2, CHUNKS):
+                words_by_scalar(c, a)
 
         two = FIRST[2]
         for tiles in (range(two), range(two, BANKS)):
@@ -239,12 +239,15 @@ def tile_mix_lrbwd_res_kernel(tc, dy, w8_words, w8_scales, bu, ad, res, out_0, o
             for a in range(1, PASSES):
                 for i in tiles:
                     base(i, a)
-        add_res_beside(two)
+        for c in range(last):
+            add_res_beside(FIRST[c])
         for i, (c, s) in enumerate(TILES):
-            if i != two:
+            if s > 0 or c == last:
                 add_res(i)
             if s == ROWS[c] - 1:
                 store(c)
+                if c == 0:
+                    permute_planes(last, 0, PASSES)
             if i + BANKS < len(TILES):
                 adapter(i + BANKS)
                 for a in range(PASSES):

from contextlib import ExitStack

import concourse.mybir as mybir

N, R, K, T = 1536, 512, 1536, 512
FLOPS = 2 * T * (N * R + N * K + R * K)

F32 = mybir.dt.float32
BF16 = mybir.dt.bfloat16
I32 = mybir.dt.int32
U32 = mybir.dt.uint32
U8 = mybir.dt.uint8
E4M3 = mybir.dt.float8_e4m3fn_x4
E5M2 = mybir.dt.float8_e5m2_x4

P = 128
PACK = 4
K_PASS = P * PACK
PASSES = N // K_PASS
ROWS = (3, 3, 4, 2)
CHUNKS = len(ROWS)
FIRST = tuple(sum(ROWS[:c]) for c in range(CHUNKS))
TILES = tuple((c, s) for c in range(CHUNKS) for s in range(ROWS[c]))
BANKS = 8
LINE = 4
SCALAR_DY = 320
SCALAR_H = 192
SCALAR_BU = 48
SCALAR_AD = (None, 64, P, P)


def tile_mix_lrbwd_res_kernel(tc, dy, w8_words, w8_scales, bu, ad, res, out_0, out_1):
    nc = tc.nc

    with ExitStack() as ctx:
        keep = ctx.enter_context(tc.tile_pool(name="keep", bufs=1))
        stage = ctx.enter_context(tc.tile_pool(name="stage", bufs=3))
        psum = ctx.enter_context(tc.psum_pool(name="psum", bufs=1))
        ctx.enter_context(tc.manual_schedule())

        def chunk_cols(c):
            return slice(FIRST[c] * P, (FIRST[c] + ROWS[c]) * P)

        def load_rows(name, rows, per_partition):
            raw = keep.tile([P, per_partition, rows.shape[1]], F32, name=name, align_bytes=256)
            nc.sync.dma_start(out=raw[:], in_=rows.rearrange("(p j) w -> p j w", j=per_partition))
            return raw

        def load_passes(name, rows):
            return [load_rows("%s%d" % (name, a), rows[a * K_PASS : (a + 1) * K_PASS, :], PACK)[:] for a in range(PASSES)]

        def load_words(a):
            words = keep.tile([P, K], I32, name="w_raw%d" % a, align_bytes=256)
            nc.sync.dma_start(out=words[:], in_=w8_words[a].rearrange("p n i -> p (n i)").bitcast(I32))
            return words

        def share(dst, src, cut):
            nc.scalar.copy(out=dst[:, :cut], in_=src[:, :cut])
            if cut < dst.shape[1]:
                nc.vector.tensor_copy(out=dst[:, cut:], in_=src[:, cut:])

        def interleave(raw, scalar_cols):
            grouped = stage.tile([P, T * PACK], BF16, name="grouped", align_bytes=64)
            dst = grouped[:].rearrange("p (c i j) -> p c j i", i=LINE, j=PACK)
            share(dst, raw.rearrange("p j (c i) -> p c j i", i=LINE), scalar_cols // LINE)
            return grouped[:]

        def interleave_permuted(grouped, raw, tiles, scalar_m):
            dst = grouped.rearrange("p (s m j) -> p m j s", s=tiles, j=PACK)
            share(dst, raw.rearrange("p j (m s) -> p m j s", s=tiles), scalar_m)
            return grouped

        def quantize(name, grouped, fmt):
            codes = keep.tile([P, grouped.shape[1] // PACK], U32, name=name + "_codes", align_bytes=64)
            scales = keep.tile([P, grouped.shape[1] // PACK], U8, name=name + "_scales", align_bytes=64)
            nc.vector.quantize_mx(out=codes[:].bitcast(fmt), scales=scales[:], in_=grouped)
            return codes, scales

        def stationary_tiles(codes, scales):
            return [(codes[:, m0 : m0 + P], scales[:, m0 : m0 + P]) for m0 in range(0, codes.shape[1], P)]

        def mx_pass(acc, stationary, moving, start, stop):
            nc.tensor.matmul_mx(
                out=acc[:],
                lhsT=stationary[0].bitcast(E4M3),
                lhsT_scale=stationary[1],
                rhs=moving[0][:].bitcast(E5M2),
                rhs_scale=moving[1][:],
                start=start,
                stop=stop,
            )

        def bank(b):
            acc = psum.tile([P, T], F32, name="bank%d" % b)
            return acc

        plane_raw = keep.tile([P, PASSES * K], U8, name="plane_raw", align_bytes=256)
        nc.vector.memset(plane_raw[:].bitcast(I32), 0)
        dy_raw = load_passes("dy_raw", dy)
        bu_raw = load_passes("bu_raw", bu)
        ad_raw = load_rows("ad_raw", ad, PACK)
        w_raw = [load_words(0)]
        for r in range(4):
            nc.sync.dma_start(
                out=plane_raw[r:P:32, :].bitcast(I32).rearrange("q (a n) -> q a n", a=PASSES),
                in_=w8_scales[:, r:16:4, :].bitcast(I32).rearrange("a q n -> q a n"),
            )

        dy_q = [quantize("dy%d" % a, interleave(dy_raw[a], SCALAR_DY), E5M2) for a in range(PASSES)]
        h_acc = [bank(s) for s in range(PACK)]
        for a in range(PASSES):
            if a < PASSES - 1:
                grouped = stage.tile([P, R * PACK], BF16, name="grouped", align_bytes=64)
                bu_q = stationary_tiles(*quantize("bu%d" % a, interleave_permuted(grouped[:], bu_raw[a], PACK, SCALAR_BU), E4M3))
            else:
                src = bu_raw[a].rearrange("p j (m u s) -> p u m j s", u=2, s=2)
                halves = []
                for u, copy in enumerate((nc.vector.tensor_copy, nc.scalar.copy)):
                    half = keep.tile([P, R * PACK // 2], BF16, name="bu_half%d" % u, align_bytes=64)
                    copy(out=half[:].rearrange("p (s m j) -> p m j s", s=2, j=PACK), in_=src[:, u])
                    halves.append(half[:])
                bu_q = []
                for u, half in enumerate(halves):
                    bu_q.extend(stationary_tiles(*quantize("bu%d_%d" % (a, u), half, E4M3)))
            for s in range(PACK):
                mx_pass(h_acc[s], bu_q[s], dy_q[a], a == 0, a == PASSES - 1)
        h_sb = keep.tile([P, PACK, T], F32, name="h_sb", align_bytes=256)
        for s in range(PACK):
            nc.scalar.copy(out=h_sb[:, s, :], in_=h_acc[s][:])
        nc.sync.dma_start(out=out_1.rearrange("(p j) t -> p j t", j=PACK), in_=h_sb[:])
        h_q = quantize("h", interleave(h_sb[:], SCALAR_H), E5M2)

        w_raw.extend([load_words(a) for a in range(1, PASSES)])
        sums = [load_rows("res%d" % c, res[chunk_cols(c), :], ROWS[c]) for c in range(CHUNKS)]

        ad_grouped, ad_q, w_codes, w_planes, acc = {}, {}, {}, {}, {}

        def group_ad(c):
            grouped = keep.tile([P, ROWS[c] * P * PACK], BF16, name="ad_grouped%d" % c, align_bytes=64)
            ad_grouped[c] = interleave_permuted(grouped[:], ad_raw[:, :, chunk_cols(c)], ROWS[c], SCALAR_AD[c])

        def quantize_ad(c):
            ad_q[c] = stationary_tiles(*quantize("ad%d" % c, ad_grouped[c], E4M3))

        def permute_words(c, a, copy, word):
            codes = keep.tile([P, ROWS[c] * P], U32, name="w_codes%d_%d" % (c, a), align_bytes=64)
            copy(
                out=codes[:].bitcast(word).rearrange("p (s g i) -> p g s i", s=ROWS[c], i=LINE),
                in_=w_raw[a][:, chunk_cols(c)].bitcast(word).rearrange("p (g i s) -> p g s i", s=ROWS[c], i=LINE),
            )
            w_codes[c, a] = codes

        def words_by_vector(c, a):
            permute_words(c, a, nc.vector.tensor_copy, I32)

        def words_by_scalar(c, a):
            permute_words(c, a, nc.scalar.copy, U32)

        def permute_planes(c, a0, a1):
            wide = ROWS[c] * P
            plane = keep.tile([P, (a1 - a0) * wide], U8, name="w_plane%d_%d" % (c, a0), align_bytes=64)
            src = plane_raw[:].rearrange("p (a k) -> p a k", a=PASSES)[:, a0:a1, chunk_cols(c)]
            nc.vector.tensor_copy(
                out=plane[:].rearrange("p (a s u m) -> p u a s m", a=a1 - a0, s=ROWS[c], u=2),
                in_=src.rearrange("p a (u m s) -> p u a s m", u=2, s=ROWS[c]),
            )
            for a in range(a0, a1):
                w_planes[c, a] = plane[:, (a - a0) * wide : (a - a0 + 1) * wide]

        def adapter(i):
            c, s = TILES[i]
            acc[i] = bank((i + PACK) % BANKS)
            mx_pass(acc[i], ad_q[c][s], h_q, True, False)

        def base(i, a):
            c, s = TILES[i]
            cols = slice(s * P, (s + 1) * P)
            mx_pass(acc[i], (w_codes[c, a][:, cols], w_planes[c, a][:, cols]), dy_q[a], False, a == PASSES - 1)

        def add_res(i):
            c, s = TILES[i]
            nc.vector.tensor_tensor(out=sums[c][:, s, :], in0=acc[i][:], in1=sums[c][:, s, :], op=mybir.AluOpType.add)

        def add_res_beside(i):
            c, s = TILES[i]
            dx = keep.tile([P, T], F32, name="dx%d" % c, align_bytes=64)
            nc.scalar.copy(out=dx[:], in_=acc[i][:])
            nc.gpsimd.tensor_tensor(out=sums[c][:, s, :], in0=dx[:], in1=sums[c][:, s, :], op=mybir.AluOpType.add)

        def store(c):
            nc.sync.dma_start(out=out_0[chunk_cols(c), :].rearrange("(p s) t -> p s t", s=ROWS[c]), in_=sums[c][:])

        def group_ad_tile(s, copy):
            grouped = keep.tile([P, P * PACK], BF16, name="ad_tile%d" % s, align_bytes=64)
            copy(
                out=grouped[:].rearrange("p (m j) -> p m j", j=PACK),
                in_=ad_raw[:, :, chunk_cols(0)].rearrange("p j (m s) -> p s m j", s=ROWS[0])[:, s],
            )
            return grouped[:]

        def quantize_ad_tile(s, grouped):
            return stationary_tiles(*quantize("ad0_%d" % s, grouped, E4M3))

        second = group_ad_tile(1, nc.scalar.copy)
        ad_q[0] = quantize_ad_tile(0, group_ad_tile(0, nc.vector.tensor_copy))
        third = group_ad_tile(2, nc.vector.tensor_copy)
        ad_q[0] = ad_q[0] + quantize_ad_tile(1, second) + quantize_ad_tile(2, third)
        last = CHUNKS - 1
        group_ad(1)
        group_ad(2)
        quantize_ad(1)
        words_by_vector(0, 0)
        permute_planes(0, 0, 1)
        words_by_vector(1, 0)
        permute_planes(1, 0, 1)
        permute_planes(2, 0, 1)
        quantize_ad(2)
        for a in range(1, PASSES):
            for c in range(2):
                permute_planes(c, a, a + 1)
            for c in range(2):
                words_by_vector(c, a)
        permute_planes(2, 1, PASSES)
        words_by_scalar(2, 0)
        group_ad(last)
        quantize_ad(last)
        words_by_scalar(last, 0)
        for a in range(1, PASSES):
            for c in range(2, CHUNKS):
                words_by_scalar(c, a)

        two = FIRST[2]
        for tiles in (range(two), range(two, BANKS)):
            for i in tiles:
                adapter(i)
            for i in tiles:
                base(i, 0)
        for tiles in (range(two), range(two, BANKS)):
            for a in range(1, PASSES):
                for i in tiles:
                    base(i, a)
        for c in range(last):
            add_res_beside(FIRST[c])
        for i, (c, s) in enumerate(TILES):
            if s > 0 or c == last:
                add_res(i)
            if s == ROWS[c] - 1:
                store(c)
                if c == 0:
                    permute_planes(last, 0, PASSES)
            if i + BANKS < len(TILES):
                adapter(i + BANKS)
                for a in range(PASSES):
                    base(i + BANKS, a)
